import numpy as np, ml_dtypes
CORES = [16,18,20,22]
N = 4
BF = ml_dtypes.bfloat16
def gentries(a):
    return np.ascontiguousarray(a.reshape(8, 16, -1).transpose(0, 2, 1)).reshape(8, -1)
def gtable(e):
    e = np.asarray(e); return np.ascontiguousarray(e.reshape(8, -1, 16).transpose(0, 2, 1)).reshape(128, -1).astype(np.int32)
G, C, P, RO, YC = 128, 32, 64, 3, 32
W, LG, LC, H, M = 4096, 7, 5, 64, 32
BIG = 2 ** 24
def probes(u, k):
    return (((u * u) >> 5)[..., None] + u[..., None] * k) & (W - 1)
def base(rng):
    ring = rng.integers(0, 256, (8, 8, 64, 16)); a = rng.integers(0, 8, (N, 8, G, 1)); b = rng.integers(0, 64, (N, 8, G, 1))
    X = ring[np.arange(8)[None, :, None, None], a, (b + np.arange(C)) & 63]
    X = np.clip(X + rng.integers(-4, 5, X.shape), 0, 255)
    th = np.where(rng.random((N, 8, P)) < 0.25, rng.integers(0, 300, (N, 8, P)), rng.integers(600, 1600, (N, 8, P)))
    return X, rng.integers(1, 256, (N, 8, 16)), rng.integers(0, 2048, (N, 8, RO, P)), th
def pack(X, wt, km, th):
    X = np.ascontiguousarray(X.reshape(N, 8, G, C, 16).transpose(0, 1, 4, 2, 3)).reshape(N, 128, W)
    return {"gen0": X.astype(np.float32).astype(BF), "wt": np.ascontiguousarray(wt.reshape(N, 128, 1)).astype(np.int32),
            "km": np.stack([gtable(a.reshape(8, -1)) for a in km]), "th": np.stack([gtable(a) for a in th])}
def setup_inputs(rng):
    return pack(*base(rng))
def column(rng, w, u):
    x = rng.integers(0, 256, 16); r = (int(u) - int(np.sum(w[2:] * x[2:]))) & (W - 1); x[0] = r & 15; x[1] = r >> 4
    return x
def link(rng, Y, w, k, o, alone=False):
    c = probes(np.arange(W)[None, :], k[None, None, :])[0]
    od = np.argsort(c.reshape(-1).astype(np.int16), kind="stable"); st = np.searchsorted(c.reshape(-1)[od], np.arange(W + 1))
    for i in range(G - 1):
        if alone and i == 1: continue
        j = 2 if alone and i == 0 else i + 1
        t = C * j + int(o[i]); us = od[st[t]:st[t + 1]] // P; us = us[~np.any(c[us] == C * i + C - 1, axis=1)]
        if len(us):
            x = column(rng, w, us[int(rng.integers(0, len(us)))]); Y[i, C - 1] = x; Y[j, int(o[i])] = x
def setup_inputs_deep(rng):
    X, wt, km, th = base(rng); th = rng.integers(30, 41, th.shape); B = 8 * N; b = np.arange(B)
    X = X.reshape(B, G, C, 16); w = wt.reshape(B, 1, 16).astype(np.int32); k0 = km[:, :, 0].reshape(B, 1, P).astype(np.int32); tries = min(128, max(16, 16 * G // P))
    for i in range(G - 1):
        x = rng.integers(0, 256, (B, tries, 16), dtype=np.int32); u = (np.sum(w * x, axis=2) & (W - 1)).astype(np.int32)
        c = probes(u, k0); o = c & (C - 1); to = np.where((b % 4 == 2) & (i == 0), 2, i + 1)
        hit = ((c >> LC) == to[:, None, None]) & (o != C - 1) & ~np.any(c == C * i + C - 1, axis=2)[..., None]
        like = np.where((b % 4 == 0)[:, None, None], o, np.where((b % 4 == 2)[:, None, None], C - 1 - o, 0)) + 1
        s = np.where(hit, like, 0).reshape(B, -1); a = np.argmax(s, axis=1)
        do = (s[b, a] > 0) & ((b % 2 == 0) | (rng.random(B) < 0.9)) & ((b % 4 != 2) | (i != 1))
        bb = b[do]; aa = a[do]; xs = x[bb, aa // P]
        X[bb, i, C - 1] = xs; X[bb, to[bb], o.reshape(B, -1)[bb, aa]] = xs
    X = X.reshape(N, 8, G, C, 16)
    for g in (3, 4, 7):
        wt[:, g, 0] = 1; wt[:, g, 1] = 16
    for r in range(N): link(rng, X[r, 4], wt[r, 4], km[r, 4, 0], np.full(G, C - 2))
    k = np.arange(2048)
    for g in (3, 7):
        h = int(rng.choice(np.array([3, 5, 7, 9]))); q0 = int(np.argmin((np.arange(C) * h + 1) & (C - 1))); Y = X[:, g].copy()
        for r in range(N):
            u = h - 1 + H * int(rng.integers(0, W // H)); c = (u * u // 32 + k * u) & (W - 1)
            km[r, g, 0] = rng.choice(k[(c & (C - 1)) != C - 1], P); Y[:, r * M:(r + 1) * M, q0] = column(rng, wt[r, g], u)
        for d in range(N): link(rng, Y[d], wt[d, g], km[d, g, 1], np.full(G, C - 2) if g == 3 else 2 * rng.integers(0, C // 2, G), g == 7)
        p = (C * np.arange(G)[:, None] + h * np.arange(C)) & (W - 1)
        for r in range(N):
            kid = np.zeros((G, C, 16), np.int64)
            for d in range(N): kid[(d - r) % N::N] = Y[d, r * M:(r + 1) * M]
            X[r, g, p >> LC, p & (C - 1)] = kid
    return pack(X, wt, km, th)
def setup_inputs_edges(rng):
    X, wt, km, th = base(rng)
    th[:, 0] = 0; e = X[:, 0, :1, C - 1].copy(); X[:, 0, ::2, C - 1] = e; X[:, 0, :, ::4] = e[:, :, None]
    f = rng.integers(0, 16, (N, G, C, 1)); X[:, 1] = (np.arange(16) == f) & (rng.random((N, G, C, 1)) < 0.2); X[:, 1, :, C - 1] = 255; th[:, 1] = 4080
    k = np.arange(2048)
    for q in range(N):
        u = int(255 * np.sum(wt[q, 1])) & (W - 1); c = ((u * u >> 5) + k * u) & (W - 1)
        good = k[(c & (C - 1)) != C - 1]
        km[q, 1, 0] = rng.choice(good if len(good) else k, P)
    km[:, 2] = rng.choice(np.array([0, 1, 3, 2047]), (N, RO, P))
    X[:, 3, ::2, C - 1] = 0; X[:, 3, 0, 0] = 0
    wt[:, 4] = 255; X[:, 4] = 255 - rng.integers(0, 3, (N, G, C, 16))
    X[:, 5, :, C - 1] = rng.integers(0, 256, (N, 1, 16))
    X[:, 6] = 255 * rng.integers(0, 2, (N, G, C, 16)); th[:, 6] = 255 * rng.integers(2, 9, (N, P))
    return pack(X, wt, km, th)
def setup_inputs_far(rng):
    X, wt, km, th = base(rng); k = np.arange(2048)
    for q in range(N):
        for g in (0, 1, 2, 4, 5):
            wt[q, g, 0] |= 1; wt[q, g, 8:] = wt[q, g, :8]
            b = np.concatenate([rng.integers(110, 181, (256, 8)), rng.integers(80, 101, (256, 8))], axis=1); u = np.sum(wt[q, g] * b, axis=1) & (W - 1)
            c = probes(u[None, :], k[None, None, :])[0]
            ok = (c == W - 1) if g == 4 else (c >= 3 * W // 4) & ((c & (C - 1)) != C - 1)
            if g == 5: ok = ok & np.any(c == 0, axis=1)[:, None]
            a, m = np.nonzero(ok); s = int(rng.integers(0, len(a))); x = b[a[s]]; c = c[a[s]]; K = int(m[s]); j = int(c[K]) >> LC; o = int(c[K]) & (C - 1)
            e = rng.integers(35, 71, (G, 8)); e[G // 4:G // 2] = rng.integers(0, 35, (G // 2 - G // 4, 8))
            if g > 2: e[:] = 0
            last = x + np.concatenate([e, -e], axis=1); X[q, g, :, C - 1] = last; km[q, g, 0] = K
            if g == 1:
                km[q, 1, 0] = rng.choice(k[(c & (C - 1)) != C - 1], P); th[q, 1] = rng.integers(2048, 4081, P)
                X[q, 1, :, :C - 1, :8] = rng.integers(0, 41, (G, C - 1, 8)); X[q, 1, :, :C - 1, 8:] = rng.integers(215, 256, (G, C - 1, 8))
            elif g == 4:
                d = rng.integers(1, 60, 16); X[q, 4, G - 1, C - 1] = x - d; th[q, 4] = int(np.sum(d)) + 1
            elif g == 5:
                d = rng.integers(1, 30, 16); X[q, 5, 0, 0] = x - d; X[q, 5, j, o] = x - rng.integers(30, 60, 16)
                km[q, 5, 0, ::2] = int(np.argmax(c == 0)); th[q, 5] = 4080; th[q, 5, ::2] = int(np.sum(d))
            else:
                v = np.repeat(np.array([0, 255]), 8); X[q, g, j, o] = v
                th[q, g] = 4080 if g == 0 else int(np.min(np.sum(np.abs(last - v), axis=1)))
    X[:, 3] = 255 - rng.integers(0, 64, (N, G, C, 16)); X[:, 3, :, C - 1] = rng.integers(0, 64, (N, G, 16)); th[:, 3] = rng.integers(2048, 4081, (N, P))
    return pack(X, wt, km, th)
def setup_inputs_spread(rng):
    X, wt, km, th = base(rng)
    X = np.minimum((rng.random((N, 8, G, C, 16)) * np.exp2(rng.integers(0, 9, (N, 8, G, C, 1)))).astype(np.int64), 255)
    wt = np.clip(np.exp2(8 * rng.random(wt.shape)).astype(np.int64), 1, 255); km = np.clip(np.exp2(11 * rng.random(km.shape)).astype(np.int64) - 1, 0, 2047); km[..., ::2] = rng.integers(0, 2048, km[..., ::2].shape)
    th = rng.integers(0, 4081, th.shape)
    return pack(X, wt, km, th)
def setup_inputs_ties(rng):
    X, wt, km, th = base(rng)
    pat = rng.integers(1, 254, (8, 4, 16)); a = rng.integers(0, 4, (N, 8, G, C))
    X = pat[np.arange(8)[None, :, None, None], a] + rng.integers(0, 2, (N, 8, G, C, 16)); th = rng.integers(3, 11, th.shape)
    return pack(X, wt, km, th)
def check_inputs(d):
    bad = []; v = np.asarray(d["gen0"]).astype(np.float32)
    if not np.all((v >= 0) & (v <= 255) & (v == np.floor(v))): bad.append("gen0 holds other numbers than 0 .. 255")
    for k, lo, hi in (("wt", 1, 255), ("km", 0, 2047), ("th", 0, 4080)):
        if np.min(d[k]) < lo or np.max(d[k]) > hi: bad.append("range of " + k)
    return bad
def reference(gen0, wt, km, th):
    B = 8 * N; X = gen0.astype(np.float32).astype(np.int32).reshape(B, 16, W); w = wt.astype(np.int64).reshape(B, 16, 1)
    kl = np.stack([gentries(a) for a in km]).astype(np.int64).reshape(B, RO, P); tl = np.stack([gentries(a) for a in th]).astype(np.int64).reshape(B, 1, P)
    ar = np.arange(G); q = np.arange(C); rows = np.arange(B)[:, None]
    for t in range(RO):
        x = X[:, :, C - 1::C]
        u = np.sum(w * x, axis=1) & (W - 1)
        c = probes(u, kl[:, t][:, None, :])
        pr = np.take_along_axis(X, c.reshape(B, 1, G * P), 2).reshape(B, 16, G, P)
        D = np.sum(np.abs(pr - x[..., None]), axis=1).astype(np.int64)
        best = np.min(np.where(D < tl, D * W + c, BIG), axis=2)
        j = (best & (W - 1)) >> LC; o = best & (C - 1); ok = (best < BIG) & (j > ar)
        acc = np.full((B, G), BIG, np.int64)
        np.minimum.at(acc, (rows, np.where(ok, j, 0)), np.where(ok, (best - (best & (W - 1))) + ar * C + o, BIG))
        got = acc < BIG; cut = np.where(got, 1 + ((acc & (C - 1)) >> 1), 0); ln = C - cut
        root = np.where(got, (acc & (W - 1)) >> LC, ar)
        for _ in range(LG): root = np.take_along_axis(root, root, 1)
        od = np.argsort(root * G + ar, axis=1)
        ls = np.take_along_axis(ln, od, 1); pos = np.zeros((B, G), np.int64)
        np.put_along_axis(pos, od, np.add.accumulate(ls, axis=1) - ls, 1); L = np.sum(ln, axis=1)
        place = np.where(q < cut[..., None], W, pos[..., None] + q - cut[..., None])
        src = np.zeros((B, W + 1), np.int64); np.put_along_axis(src, place.reshape(B, W), np.arange(W)[None, :], 1)
        p = ((ar * L[:, None]) >> LG)[..., None] + q * (1 + (u & (H - 1)))[..., None]
        p = np.where(p >= L[:, None, None], p - L[:, None, None], p)
        col = np.take_along_axis(src, p.reshape(B, W), 1)
        kid = np.take_along_axis(X, col[:, None, :], 2).reshape(N, 8, 16, G, C); nxt = np.empty_like(kid)
        for r in range(N):
            for d in range(N): nxt[d, :, :, r * M:(r + 1) * M] = kid[r, :, :, (d - r) % N::N]
        X = nxt.reshape(B, 16, W)
    return {"y": np.ascontiguousarray(X.reshape(N, 128, G, C)[..., :YC]).reshape(N, 128, G * YC).astype(np.float32).astype(BF)}

@@ -1,0 +1,457 @@
+from concourse.mybir import AluOpType, AxisListType, ActivationFunctionType
+
+A = AluOpType
+F = ActivationFunctionType
+N = 4
+MB = 1024
+BANKS = (("b2", (7, 6)), ("b3", (5, 4)), ("b4", (3, 2, 1, 0)))
+SEG = {}
+for _bank, _js in BANKS:
+    _c = 0
+    for _j in _js:
+        SEG[_j] = (_bank, _c, 16 * (_j + 1))
+        _c += 16 * (_j + 1)
+BANKW = {"b2": 240, "b3": 176, "b4": 160}
+CTO = {"b2": 0, "b3": 240, "b4": 416}
+SCH = [(0, 8), (8, 12)]
+VCH = [(12, 20), (20, 28), (28, 36), (36, 44), (44, 52), (52, 58), (58, 62), (62, 64)]
+LATE = 58
+LAYS = 144
+
+_f, _h, _b, _i, _u = "float32", "float16", "bfloat16", "int32", "uint16"
+_sb = {
+    _b: "x0:4096 x1:4096 x2:4096 x3:4096 lay:4096 ko0:3072 ko1:3072 ko2:3072 q16:128 q17:128 bq:128 bo:128 bo27:128 "
+        "mk2:256 idb:128 nid:128 ld:2048 ws:2048 bw:128 ones:128 omi:128 gsel:1024 grp:1024 jt:512 kcol:8 rst:128 "
+        "xrep:1024 ga:2048 d:8192 ab:8192 gd:512 ej:128 ef:128 el:128 mm:128 lb:1024 cmp:1024 "
+        "f0:128 f1:128 f2:128 f3:128 f4:128 f5:128 f6:128 f7:128",
+    _h: "bo12:128 boh:128 idh:128 c16:512 ed:256",
+    _f: "wtf:1 wtf1:1 ekt:256 kr:192 th2:512 pf:1 pm:1 pm16:1 pg:1 row:128 mg:128 bof:128 idf:128 i16:8 i1:8 gc:8 "
+        "pgc:8 negr:8 jtf:512 kc:512 il:8 eq0:8 tgt:8 tc:8 ct:576 self:8 ioc:8 pl:256 kperm:128 ac:128 uf:8 u2:8 "
+        "mk:512 bf:8 jm:8 accf:8 sc:128 lc:1 pp:256 pw:256 mp:128 t4:128 vrow:128 sp:128 wb:264 w1:256 ff:256",
+    _i: "wti:1 kt:16 pi:1 pmi:1 pgi:1 expi:16 ui:8 ub:8 sq:8 s5:8 cv:512 ci:512 best:8 jI:8 dI:8 oI:8 jv:8 dio:16 "
+        "acc:8 fI:8 cI:8 lI:8 hI:128 h63:128 kl:128 sk:128 cell:8 si:256 sj:256",
+    _u: "expl:16 cl:512 plist:256 celll:8 sl:256 fl0:8 fl1:8 fl2:8 fl3:8 fl4:8 fl5:8 fl6:8",
+}
+WIDTH, TYPE, PLACE, SCRATCH, _used = {}, {}, {}, {}, {}
+for _t, _list in _sb.items():
+    for _e in _list.split():
+        _k, _w = _e.split(":")
+        WIDTH[_k], TYPE[_k], PLACE[_k] = int(_w), _t, (_k, 0)
+        if int(_w) <= 16 and _k not in ("wti", "kt"):
+            PLACE[_k] = ("small_" + _t, _used.get(_t, 0))
+            _used[_t] = _used.get(_t, 0) + 16
+        else:
+            SCRATCH[_k] = ("sbuf", [128, int(_w)], _t)
+for _k, _v in _used.items():
+    SCRATCH["small_" + _k] = ("sbuf", [128, _v], _k)
+for _k in range(8):
+    SCRATCH["b%d" % _k] = ("psum", [128, 512], _f)
+    WIDTH["b%d" % _k], TYPE["b%d" % _k], PLACE["b%d" % _k] = 512, _f, ("b%d" % _k, 0)
+SEMAPHORES = ["qV", "qS", "qP", "qG"] + ["dl%d" % k for k in range(12)] + \
+    ["ar%d_%d" % (t, k) for t in range(3) for k in range(4)] + ["ls%d" % t for t in range(3)]
+
+
+def build_tracker(g, T):
+    eng = {"V": g.vector, "S": g.scalar, "P": g.tensor, "G": g, "Y": g.sync}
+    cnt = {"V": 0, "S": 0, "P": 0, "G": 0}
+    clk = {q: {} for q in eng}
+    snap = {}
+    acc = {}
+    ndma = [0]
+
+    def meet(r, e):
+        if r[1] >= e[3] or e[2] >= r[2]:
+            return False
+        return not (r[3] == e[4] and r[3] > 1 and (r[1] - e[2]) % r[3])
+
+    def sync(q, outs, ins):
+        need = {}
+        for w, regs in ((True, outs), (False, ins)):
+            for r in regs:
+                psum = SCRATCH[r[0]][0] == "psum"
+                for e in acc.get(r[0], ()):
+                    if e[0] != q:
+                        hit = psum or ((w or e[5]) and meet(r, e))
+                    else:
+                        hit = e[5] and q != "P" and meet(r, e)
+                    tok = e[1]
+                    if hit and clk[q].get(tok[0], 0) < tok[1] and need.get(tok[0], 0) < tok[1]:
+                        need[tok[0]] = tok[1]
+        items = sorted(need.items(), key=lambda kv: kv[0])
+        for s, v in items:
+            if not any(s2 != s and snap[(s2, v2)].get(s, 0) >= v for s2, v2 in items):
+                eng[q].wait_ge(T.sem[s], v)
+        for tok in items:
+            for s, v in snap[tok].items():
+                clk[q][s] = max(v, clk[q].get(s, 0))
+
+    def note(q, tok, outs, ins):
+        for w, regs in ((True, outs), (False, ins)):
+            for r in regs:
+                lst = acc.setdefault(r[0], [])
+                lst[:] = [e for e in lst if not (e[0] == q and (e[5] == w or w) and e[2] >= r[1] and e[3] <= r[2]
+                                                 and (r[3] == 1 or (e[4] == r[3] and (e[2] - r[1]) % r[3] == 0)))]
+                lst.append((q, tok, r[1], r[2], r[3], w))
+
+    def done(q, who, tok, outs, ins):
+        snap[tok] = dict(clk[q]) if q else {}
+        snap[tok][tok[0]] = tok[1]
+        note(who, tok, outs, ins)
+
+    def emit(q, call, outs, ins):
+        sync(q, outs, ins)
+        cnt[q] += 1
+        call(eng[q]).then_inc(T.sem["q" + q], 1)
+        done(q, q, ("q" + q, cnt[q]), outs, ins)
+
+    def dma(q, out_ap, in_ap, outs, ins):
+        sync(q, outs, ins)
+        s = "dl%d" % ndma[0]
+        ndma[0] += 1
+        eng[q].dma_start(out_ap, in_ap).then_inc(T.sem[s], 16)
+        done(q, s, (s, 16), outs, ins)
+
+    def arrive(s, val, outs):
+        done(None, s, (s, val), outs, ())
+
+    def finish(extra):
+        for q in ("V", "S", "P", "G"):
+            g.wait_ge(T.sem["q" + q], cnt[q])
+        for k in range(ndma[0]):
+            g.wait_ge(T.sem["dl%d" % k], 16)
+        for s, v in extra:
+            g.wait_ge(T.sem[s], v)
+    return emit, dma, sync, arrive, finish
+
+
+def rank_program(g, core, T, topo):
+    rank = T.rank_of(core)
+    if rank is None:
+        return
+    emit, dma, sync, arrive, finish = build_tracker(g, T)
+
+    def R(name, a=0, b=None, st=1):
+        p, o = PLACE[name]
+        return (p, o + a, o + (WIDTH[name] if b is None else b), st)
+
+    def blk(name, k, w=128):
+        return R(name, w * k, w * k + w)
+
+    def ap(r):
+        if r[3] == 1:
+            return T[r[0]][:, r[1]:r[2]]
+        return T[r[0]][:, r[1]:r[2]:r[3]]
+
+    def src(r, idx):
+        return ap(r) if idx is None else ap(r).indirect(ap(idx))
+
+    def regs(*rs):
+        return [r for r in rs if isinstance(r, tuple)]
+
+    def sca(v):
+        return ap(v) if isinstance(v, tuple) else v
+
+    def tt(out, in0, in1, op, idx=None):
+        emit("V", lambda e: e.tensor_tensor(ap(out), src(in0, idx), ap(in1), op), [out], regs(in0, in1, idx))
+
+    def ts(out, in0, s1, s2, op0, op1=None):
+        if op1 is None:
+            emit("V", lambda e: e.tensor_scalar(ap(out), ap(in0), sca(s1), None, op0), [out], regs(in0, s1))
+        else:
+            emit("V", lambda e: e.tensor_scalar(ap(out), ap(in0), sca(s1), sca(s2), op0, op1), [out], regs(in0, s1, s2))
+
+    def cp(out, in_, idx=None, oidx=None):
+        emit("V", lambda e: e.tensor_copy(src(out, oidx), src(in_, idx)), [out], regs(in_, idx, oidx))
+
+    def fill(out, v):
+        emit("V", lambda e: e.memset(ap(out), v), [out], [])
+
+    def red(out, in_, op, absv=False):
+        emit("V", lambda e: e.tensor_reduce(ap(out), ap(in_), AxisListType.X, op, apply_absolute_value=absv), [out], [in_])
+
+    def scan(out, d0, d1, init, op0, op1):
+        emit("V", lambda e: e.tensor_tensor_scan(ap(out), ap(d0), ap(d1), sca(init), op0, op1), [out], regs(d0, d1, init))
+
+    def act(out, in_, fn, idx=None, scale=None, bias=None):
+        kw = {}
+        if scale is not None:
+            kw["scale"] = sca(scale)
+        if bias is not None:
+            kw["bias"] = ap(bias)
+        emit("S", lambda e: e.activation(ap(out), src(in_, idx), fn, **kw), [out], regs(in_, idx, scale, bias))
+
+    def mm(out, lhsT, rhs, start, stop):
+        emit("P", lambda e: e.matmul(ap(out), ap(lhsT), ap(rhs), start, stop), [out], [lhsT, rhs])
+
+    def iota(name, pattern, cm=0):
+        out = R(name)
+        kw = {} if TYPE[name] == _i else {"allow_small_or_imprecise_dtypes": True}
+        emit("G", lambda e: e.iota(ap(out), pattern, 0, cm, **kw), [out], [])
+
+    dma("Y", T.x0[:], T.gen0[:], [R("x0")], [])
+    dma("S", T.kt[:, 0:12], T.km[:], [R("kt", 0, 12)], [])
+    dma("S", T.kt[:, 12:16], T.th[:], [R("kt", 12, 16)], [])
+    dma("S", T.wti[:], T.wt[:], [R("wti")], [])
+
+    iota("pi", [[0, 1]], 1)
+    iota("q16", [[0, 8], [1, 16]])
+    iota("mg", [[1, 8], [0, 16]])
+    iota("expi", [[1, 16]])
+    iota("row", [[1, 128]])
+    iota("i16", [[16, 8]])
+    iota("i1", [[1, 8]])
+    iota("kperm", [[1, 4], [4, 32]])
+    iota("jtf", [[0, 4], [1, 128]])
+    iota("pl", [[16, 256]])
+    MK = R("mk2", 0, 128)
+    E8 = R("expl", 0, 8)
+    cp(R("pf"), R("pi"))
+    ts(R("pmi"), R("pi"), 15, None, A.bitwise_and)
+    ts(R("pgi"), R("pi"), 4, None, A.arith_shift_right)
+    cp(R("expl"), R("expi"))
+    cp(R("pm"), R("pmi"))
+    cp(R("pg"), R("pgi"))
+    ts(R("q17"), R("q16"), 1.0, None, A.add)
+    ts(R("bo"), R("mg"), R("pg"), None, A.is_equal)
+    ts(R("bof"), R("mg"), R("pg"), None, A.is_equal)
+    ts(MK, R("q16"), R("pm"), None, A.is_equal)
+    ts(R("mk2", 128, 256), R("q16"), R("pm"), None, A.is_equal)
+    tt(R("bq"), R("q17"), R("bo"), A.mult)
+    for s in range(16):
+        ts(blk("ld", s), R("bq"), float(s + 1), 4096.0, A.is_equal, A.mult)
+    ts(R("wtf"), R("wti"), 1.0 / 4096.0, None, A.mult)
+    for s in range(4):
+        act(blk("ws", s, 512), blk("ld", s, 512), F.Copy, None, R("wtf"))
+    ts(R("wtf1"), R("wti"), 1.0, None, A.mult)
+    ts(R("bw"), R("bo"), R("wtf1"), None, A.mult)
+    tt(R("ekt"), R("kt"), R("mk2"), A.mult, R("expl"))
+    mm(R("b1", 0, 256), R("bof"), R("ekt"), True, True)
+    ts(R("idf"), R("row"), R("pf"), None, A.is_equal)
+    ts(R("idb"), R("row"), R("pf"), None, A.is_equal)
+    ts(R("nid"), R("row"), R("pf"), -1.0, A.is_equal, A.mult)
+    ts(R("idh"), R("row"), R("pf"), None, A.is_equal)
+    fill(R("kc"), 2048.0 - 2.0 ** 24)
+    cp(R("kr"), R("b1", 0, 192))
+    for k in range(8):
+        ts(R("th2", k, 512, 8), R("b1", 192, 256), 4096.0, -(2.0 ** 24), A.mult, A.add)
+
+    def later_constants():
+        fill(R("ones"), 1.0)
+        ts(R("il"), R("i16"), R("pm"), None, A.add)
+        ts(R("pgc"), R("i1"), R("pg"), None, A.is_equal)
+        ts(R("eq0"), R("il"), 0.0, None, A.is_equal)
+        tt(R("tgt"), R("il"), R("eq0"), A.subtract)
+        ts(R("tc"), R("tgt"), -(2.0 ** 27), 2.0 ** 23 + 2048.0, A.mult, A.add)
+        ts(R("gc"), R("i16"), R("pf"), 128.0, A.is_equal, A.mult)
+        ts(R("pm16"), R("pm"), 16.0, None, A.add)
+        ts(R("self"), R("il"), 32.0, 4095.0 * 4096.0, A.mult, A.add)
+        ts(R("ioc"), R("il"), 32.0, 1.0 - 2048.0, A.mult, A.add)
+        for k in range(8):
+            bank, c, w = SEG[k]
+            ts(R("ct", CTO[bank] + c, CTO[bank] + c + w), R("ones", 0, w), R("tc", k, k + 1), None, A.mult)
+        for k in range(8):
+            ts(blk("grp", k), R("bo"), R("pgc", k, k + 1), 1.0 if k < 4 else 0.5, A.mult, A.mult)
+            ts(blk("gsel", k), R("ones"), R("gc", k, k + 1), None, A.mult)
+        ts(R("omi"), R("row"), R("pf"), None, A.not_equal)
+        ts(R("bo27"), R("bo"), 2.0 ** 27, None, A.mult)
+        ts(R("bo12"), R("bo"), 4096.0, None, A.mult)
+        ts(R("boh"), R("bo"), 1.0, None, A.mult)
+        ts(R("kcol"), R("ones", 0, 8), R("pf"), None, A.mult)
+        ts(R("rst"), R("q16"), 0.0, None, A.is_gt)
+        ts(R("jt"), R("jtf"), 1.0 / 128.0, None, A.mult)
+        ts(R("ac"), R("row"), 32.0, 32.0, A.mult, A.add)
+        ts(R("b1", 256, 512), R("pl"), R("pm"), None, A.add)
+        ts(R("b1", 0, 256), R("b1", 256, 512), 1.0, 4095.0, A.add, A.mult)
+    extra = []
+
+    for t in range(3):
+        X = "x%d" % t
+        Xn = "x%d" % (t + 1)
+        ko = "ko%d" % t
+        for s in range(16):
+            mm(R("b4", 0, 8), blk("ws", s), R(X, 32 * s + 31, 4096, 512), s == 0, s == 15)
+        for k in range(4):
+            mm(blk("b5", k, 32), R("bw"), R(X, 32 * k + 31, 4096, 128), True, True)
+        mm(R("b0"), R("idf"), R("kc"), True, False)
+        act(R("xrep", 0, 128), R(X, 31, 4096, 32), F.Copy)
+        for w in (128, 256, 512):
+            act(R("xrep", w, 2 * w), R("xrep", 0, w), F.Copy)
+        cp(R("ui"), R("b4", 0, 8))
+        ts(R("ub"), R("ui"), 4095, None, A.bitwise_and)
+        tt(R("sq"), R("ub"), R("ub"), A.mult)
+        cp(R("uf"), R("ub"))
+        ts(R("s5"), R("sq"), 5, None, A.arith_shift_right)
+        cp(R("u2"), R("s5"))
+        for k in range(8):
+            ts(R("cv", k, 512, 8), blk("kr", t, 64), R("uf", k, k + 1), R("u2", k, k + 1), A.mult, A.add)
+        for a, b in ((0, 160), (160, 512)):
+            ts(R("ci", a, b), R("cv", a, b), 4095, None, A.bitwise_and)
+            cp(R("cl", a, b), R("ci", a, b))
+
+        def gather_s(k):
+            m0, m1 = SCH[k]
+            act(R("ga", 128 * m0, 128 * m1), R(X), F.Copy, R("cl", 8 * m0, 8 * m1))
+            for c in range(m0 // 4, m1 // 4):
+                bank = R("b%d" % (6 + c % 2))
+                mm(bank, R("idb"), blk("ga", c, 512), True, False)
+                mm(bank, R("nid"), R("xrep", 0, 512), False, True)
+
+        def abs_s(k):
+            for c in range(SCH[k][0] // 4, SCH[k][1] // 4):
+                act(blk("ab", c, 512), R("b%d" % (6 + c % 2)), F.Abs)
+
+        def dist(m0, m1, stop):
+            if m0 >= LATE:
+                out = R("b7", 8 * (m0 - LATE), 8 * (m1 - LATE))
+            else:
+                out = R("b0", 8 * m0, 8 * m1)
+            for s in range(16):
+                mm(out, blk("ld", s), R("ab", 128 * m0 + s, 128 * m1, 16), False, stop and s == 15)
+
+        e = 8 * LATE
+        gather_s(0)
+        for k, (m0, m1) in enumerate(VCH):
+            tt(R("d", 128 * m0, 128 * m1), R(X), R("xrep", 0, 128 * (m1 - m0)), A.subtract, R("cl", 8 * m0, 8 * m1))
+            if k < 2:
+                abs_s(k)
+                if k == 0:
+                    gather_s(1)
+            act(R("ab", 128 * m0, 128 * m1), R("d", 128 * m0, 128 * m1), F.Abs)
+            if k == 1:
+                ts(R("c16"), R("cl"), -2048.0, None, A.add)
+                mm(R("b0"), R("idh"), R("c16"), False, False)
+                dist(SCH[0][0], SCH[0][1], False)
+                dist(VCH[0][0], VCH[0][1], False)
+                dist(SCH[1][0], SCH[1][1], False)
+                mm(R("b7", 0, 512 - e), R("idf"), R("kc", e, 512), True, False)
+                mm(R("b7", 0, 512 - e), R("idh"), R("c16", e, 512), False, False)
+            if k >= 1:
+                dist(m0, m1, m1 == LATE or m1 == 64)
+        if t == 0:
+            later_constants()
+        for bank, js in BANKS:
+            mm(R(bank, 0, BANKW[bank]), R("idf"), R("ct", CTO[bank], CTO[bank] + BANKW[bank]), True, False)
+        cp(R("hI"), R("b5", 0, 128))
+        ts(R("h63"), R("hI"), 63, None, A.bitwise_and)
+        fill(R("wb"), 0.0)
+        for bank, a, b in (("b0", 0, e), ("b7", e, 512)):
+            tt(R("gd", a, b), R(bank, 0, b - a), R("th2", a, b), A.is_lt)
+            tt(R("mk", a, b), R(bank, 0, b - a), R("gd", a, b), A.mult)
+        for k in range(8):
+            red(R("bf", k, k + 1), R("mk", k, 512, 8), A.min)
+        cp(R("best"), R("bf"))
+        ts(R("jI"), R("best"), 5, 127, A.arith_shift_right, A.bitwise_and)
+        ts(R("dI"), R("best"), 12, None, A.arith_shift_right)
+        ts(R("oI"), R("best"), 1, 15, A.arith_shift_right, A.bitwise_and)
+        tt(R("jm"), R("jI"), R("il"), A.is_gt)
+        ts(R("dio", 0, 8), R("dI"), 2048.0, None, A.add)
+        tt(R("dio", 8, 16), R("oI"), R("ioc"), A.add)
+        tt(R("jv"), R("jI"), R("jm"), A.mult)
+        tt(R("ej"), R("jv"), MK, A.mult, E8)
+        tt(R("ed"), R("dio"), R("mk2"), A.mult, R("expl"))
+        for bank, js in BANKS:
+            seg = {j: R(bank, SEG[j][1], SEG[j][1] + SEG[j][2]) for j in js}
+            for j in js:
+                mm(seg[j], R("bo27"), R("ej", 0, SEG[j][2]), False, False)
+            for j in js:
+                mm(seg[j], R("bo12"), R("ed", 0, SEG[j][2]), False, False)
+                mm(seg[j], R("boh"), R("ed", 128, 128 + SEG[j][2]), False, j == js[-1])
+        ts(blk("b0", 0), R("h63"), 1.0, R("pm"), A.add, A.mult)
+        ts(blk("b0", 1), R("h63"), 1.0, R("pm16"), A.add, A.mult)
+        for bank, js in BANKS:
+            for j in js:
+                red(R("accf", j, j + 1), R(bank, SEG[j][1], SEG[j][1] + SEG[j][2]), A.min, True)
+        tt(R("acc"), R("accf"), R("self"), A.min)
+        ts(R("fI"), R("acc"), 5, 127, A.arith_shift_right, A.bitwise_and)
+        ts(R("cI"), R("acc"), 31, None, A.bitwise_and)
+        tt(R("ef"), R("fI"), MK, A.mult, E8)
+        mm(R("b5", 0, 128), R("bo"), R("ef"), True, True)
+        cp(R("fl0"), R("fI"))
+        act(R("f0"), R("b5", 0, 128), F.Copy)
+        ts(R("lI"), R("cI"), -1.0, 32.0, A.mult, A.add)
+        tt(R("el"), R("lI"), MK, A.mult, E8)
+        mm(R("b4", 0, 128), R("bo"), R("el"), True, True)
+        mm(R("b6"), R("el"), R("grp", 0, 512), True, True)
+        mm(R("b7"), R("el"), R("grp", 512, 1024), True, True)
+        mm(R("b2"), blk("gsel", 0), R("jt"), True, False)
+        mm(R("b3"), blk("gsel", 0), R("jt"), True, False)
+        gaps = [
+            lambda: red(R("lc"), R("b4", 0, 128), A.add),
+            lambda: ts(R("kl"), R("kperm"), R("lc"), None, A.mult),
+            lambda: ts(R("sk"), R("kl"), 7, None, A.arith_shift_right),
+            lambda: tt(R("pp", 0, 256, 2), R("sk"), blk("b0", 0), A.add),
+            lambda: tt(R("pp", 1, 256, 2), R("sk"), blk("b0", 1), A.add),
+            lambda: None,
+        ]
+        for k in range(6):
+            fk = R("f%d" % k)
+            fl = R("fl%d" % k)
+            tt(R("mm"), fk, MK, A.mult, fl)
+            act(R("f%d" % (k + 1)), fk, F.Copy, fl)
+            if k < 4:
+                act(blk("lb", k, 256), blk("b%d" % (6 + k // 2), k % 2, 256), F.Copy)
+            gaps[k]()
+            scan(R("sc"), R("rst"), R("mm"), 0.0, A.mult, A.add)
+            cp(R("fl%d" % (k + 1)), R("sc", 15, 128, 16))
+        tt(R("b6", 0, 128), R("ac"), R("b4", 0, 128), A.subtract)
+        mm(R("b4", 0, 8), R("idb"), R("kcol"), True, False)
+        act(R("f7"), R("f6"), F.Copy, R("fl6"))
+        ts(R("b6", 256, 512), R("pp"), R("lc"), R("lc"), A.is_ge, A.mult)
+        tt(R("pw"), R("pp"), R("b6", 256, 512), A.subtract)
+        mm(R("b4", 0, 8), R("f7"), R("gsel", 0, 1024, 128), False, True)
+        act(R("negr", 4, 8), R("b4", 4, 8), F.Copy, None, -1.0)
+        order = (4, 5, 6, 7, 0, 1, 2, 3)
+        for k in order:
+            mm(blk("b2" if k < 4 else "b3", k % 4), blk("gsel", k), R("f7"), False, k % 4 == 3)
+        for k in range(4, 8):
+            mm(R("b5", 0, 128), blk("lb", k), R("omi"), k == 4, False)
+        for k in order:
+            if k < 4:
+                ts(blk("cmp", k), blk("b2", k), R("b4", k, k + 1), None, A.is_gt)
+            else:
+                act(blk("cmp", k), blk("b3", k % 4), F.Sign, None, None, R("negr", k, k + 1))
+        for k in (0, 1, 4, 5, 2, 3, 6, 7):
+            mm(R("b5", 0, 128), blk("lb", k), blk("cmp", k), False, k == 7)
+        cp(R("plist"), R("pw"))
+        tt(R("mp"), R("b5", 0, 128), MK, A.mult)
+        ts(R("t4"), R("b5", 0, 128), 4095.0, None, A.mult)
+        scan(R("sp"), R("rst"), R("mp"), 0.0, A.mult, A.add)
+        tt(R("vrow"), R("t4"), R("b6", 0, 128), A.add)
+        ts(R("cell"), R("sp", 15, 128, 16), 0.0625, -0.46875, A.mult, A.add)
+        cp(R("celll"), R("cell"))
+        cp(R("wb", 8, 264), R("vrow"), None, R("celll"))
+        for a, b in ((0, LAYS), (LAYS, 256)):
+            tt(R("b7", a, b), R("wb", 8 + a, 8 + b), R("b1", a, b), A.is_lt)
+            tt(R("w1", a, b), R("wb", 8 + a, 8 + b), R("b7", a, b), A.mult)
+            scan(R("ff", a, b), R("wb", 7 + a, 7 + b), R("w1", a, b), R("ff", a - 1, a) if a else 0.0, A.max, A.max)
+            tt(R("si", a, b), R("ff", a, b), R("b1", 256 + a, 256 + b), A.add)
+            ts(R("sj", a, b), R("si", a, b), 4095, None, A.bitwise_and)
+            cp(R("sl", a, b), R("sj", a, b))
+            if a:
+                cp(R("lay", 16 * a, 4096), R(X), R("sl", a, b))
+            else:
+                act(R("lay", 0, 16 * b), R(X), F.Copy, R("sl", a, b))
+        o = MB * rank
+        for q, kr, a, b in (("V", 1, 0, 64), ("S", 3, 0, 64), ("V", 2, 0, 32), ("S", 2, 32, 64),
+                            ("V", 0, 0, 32), ("S", 0, 32, 64)):
+            to = R(Xn, o + 16 * a, o + 16 * b)
+            out = R(ko, MB * (kr - 1) + 16 * a, MB * (kr - 1) + 16 * b) if kr else to
+            lst = R("plist", 64 * kr + a, 64 * kr + b)
+            if q == "V":
+                cp(out, R("lay"), lst)
+            else:
+                act(out, R("lay"), F.Copy, lst)
+            if kr:
+                dst = T.cores[(kr + rank) % N]
+                rid, pid, _ = topo.addr(dst)
+                sync("G", [], [out])
+                g.remote_dma(out_ap=ap(to), in_ap=ap(out), remote_sem=T.sem["ar%d_%d" % (t, kr)],
+                             local_sem=T.sem["ls%d" % t], pid=pid, routing_id=rid, dma_engine_mask=topo.mask(core, dst))
+        ne = len(topo.engines(core, T.cores[(rank + 1) % N]))
+        extra.append(("ls%d" % t, 4 * ne))
+        for kr in (1, 2, 3):
+            arrive("ar%d_%d" % (t, kr), ne * (2 if kr == 2 else 1), [blk(Xn, (rank - kr) % N, MB)])
+    for kr in (0, 1, 3, 2):
+        s = (rank - kr) % N
+        dma("Y", T.y[:, MB * s:MB * s + MB], T.x3[:, MB * s:MB * s + MB], [], [blk("x3", s, MB)])
+    finish(extra)

@@ -1,3 +1,4 @@
+from concourse.bass import DstId, RemoteDMATransfer
 from concourse.mybir import AluOpType, AxisListType, ActivationFunctionType
 
 A = AluOpType
@@ -16,21 +17,21 @@ CTO = {"b2": 0, "b3": 240, "b4": 416}
 SCH = [(0, 8), (8, 12)]
 VCH = [(12, 20), (20, 28), (28, 36), (36, 44), (44, 52), (52, 58), (58, 62), (62, 64)]
 LATE = 58
-LAYS = 144
+LAYS = 148
 
 _f, _h, _b, _i, _u = "float32", "float16", "bfloat16", "int32", "uint16"
 _sb = {
     _b: "x0:4096 x1:4096 x2:4096 x3:4096 lay:4096 ko0:3072 ko1:3072 ko2:3072 q16:128 q17:128 bq:128 bo:128 bo27:128 "
-        "mk2:256 idb:128 nid:128 ld:2048 ws:2048 bw:128 ones:128 omi:128 gsel:1024 grp:1024 jt:512 kcol:8 rst:128 "
+        "mk2:256 idb:128 nid:128 ld:2048 bw:128 ones:128 omi:128 gsel:1024 grp:1024 jt:512 kcol:8 rst:128 "
         "xrep:1024 ga:2048 d:8192 ab:8192 gd:512 ej:128 ef:128 el:128 mm:128 lb:1024 cmp:1024 "
-        "f0:128 f1:128 f2:128 f3:128 f4:128 f5:128 f6:128 f7:128",
+        "f0:128 f1:128 f2:128 f3:128 f4:128 f7:128 h0:128 h1:128 h2:128 h3:128",
     _h: "bo12:128 boh:128 idh:128 c16:512 ed:256",
-    _f: "wtf:1 wtf1:1 ekt:256 kr:192 th2:512 pf:1 pm:1 pm16:1 pg:1 row:128 mg:128 bof:128 idf:128 i16:8 i1:8 gc:8 "
+    _f: "wtf:1 ekt:256 kr:192 th2:512 pf:1 pm:1 pm16:1 pm4:1 pg:1 row:128 mg:128 bof:128 idf:128 i16:8 i1:8 gc:8 "
         "pgc:8 negr:8 jtf:512 kc:512 il:8 eq0:8 tgt:8 tc:8 ct:576 self:8 ioc:8 pl:256 kperm:128 ac:128 uf:8 u2:8 "
         "mk:512 bf:8 jm:8 accf:8 sc:128 lc:1 pp:256 pw:256 mp:128 t4:128 vrow:128 sp:128 wb:264 w1:256 ff:256",
     _i: "wti:1 kt:16 pi:1 pmi:1 pgi:1 expi:16 ui:8 ub:8 sq:8 s5:8 cv:512 ci:512 best:8 jI:8 dI:8 oI:8 jv:8 dio:16 "
         "acc:8 fI:8 cI:8 lI:8 hI:128 h63:128 kl:128 sk:128 cell:8 si:256 sj:256",
-    _u: "expl:16 cl:512 plist:256 celll:8 sl:256 fl0:8 fl1:8 fl2:8 fl3:8 fl4:8 fl5:8 fl6:8",
+    _u: "expl:16 cl:512 plist:256 celll:8 sl:256 fl0:8 fl1:8 fl2:8 fl3:8 fl4:8",
 }
 WIDTH, TYPE, PLACE, SCRATCH, _used = {}, {}, {}, {}, {}
 for _t, _list in _sb.items():
@@ -70,10 +71,7 @@ def build_tracker(g, T):
             for r in regs:
                 psum = SCRATCH[r[0]][0] == "psum"
                 for e in acc.get(r[0], ()):
-                    if e[0] != q:
-                        hit = psum or ((w or e[5]) and meet(r, e))
-                    else:
-                        hit = e[5] and q != "P" and meet(r, e)
+                    hit = (psum and e[0] != q) or ((w or e[5]) and (q, e[0]) != ("P", "P") and meet(r, e))
                     tok = e[1]
                     if hit and clk[q].get(tok[0], 0) < tok[1] and need.get(tok[0], 0) < tok[1]:
                         need[tok[0]] = tok[1]
@@ -177,7 +175,7 @@ def rank_program(g, core, T, topo):
         if scale is not None:
             kw["scale"] = sca(scale)
         if bias is not None:
-            kw["bias"] = ap(bias)
+            kw["bias"] = sca(bias)
         emit("S", lambda e: e.activation(ap(out), src(in_, idx), fn, **kw), [out], regs(in_, idx, scale, bias))
 
     def mm(out, lhsT, rhs, start, stop):
@@ -219,64 +217,63 @@ def rank_program(g, core, T, topo):
     tt(R("bq"), R("q17"), R("bo"), A.mult)
     for s in range(16):
         ts(blk("ld", s), R("bq"), float(s + 1), 4096.0, A.is_equal, A.mult)
-    ts(R("wtf"), R("wti"), 1.0 / 4096.0, None, A.mult)
-    for s in range(4):
-        act(blk("ws", s, 512), blk("ld", s, 512), F.Copy, None, R("wtf"))
-    ts(R("wtf1"), R("wti"), 1.0, None, A.mult)
-    ts(R("bw"), R("bo"), R("wtf1"), None, A.mult)
+    cp(R("wtf"), R("wti"))
+    ts(R("bw"), R("bo"), R("wtf"), None, A.mult)
     tt(R("ekt"), R("kt"), R("mk2"), A.mult, R("expl"))
     mm(R("b1", 0, 256), R("bof"), R("ekt"), True, True)
     ts(R("idf"), R("row"), R("pf"), None, A.is_equal)
     ts(R("idb"), R("row"), R("pf"), None, A.is_equal)
     ts(R("nid"), R("row"), R("pf"), -1.0, A.is_equal, A.mult)
     ts(R("idh"), R("row"), R("pf"), None, A.is_equal)
-    fill(R("kc"), 2048.0 - 2.0 ** 24)
-    cp(R("kr"), R("b1", 0, 192))
+    ts(R("rst"), R("q16"), 0.0, None, A.is_gt)
+    fill(R("ones"), 1.0)
+    ts(R("il"), R("i16"), R("pm"), None, A.add)
+    ts(R("pgc"), R("i1"), R("pg"), None, A.is_equal)
+    ts(R("gc"), R("i16"), R("pf"), 128.0, A.is_equal, A.mult)
+    ts(R("eq0"), R("il"), 0.0, None, A.is_equal)
+    ts(R("pm16"), R("pm"), 16.0, None, A.add)
+    ts(R("pm4"), R("pm"), 4095.0, 4095.0, A.mult, A.add)
+    tt(R("tgt"), R("il"), R("eq0"), A.subtract)
+    ts(R("pgc", 4, 8), R("pgc", 4, 8), 0.5, None, A.mult)
+    ts(R("self"), R("il"), 32.0, 4095.0 * 4096.0, A.mult, A.add)
+    ts(R("tc"), R("tgt"), -(2.0 ** 27), 2.0 ** 23 + 2048.0, A.mult, A.add)
+    ts(R("ioc"), R("il"), 32.0, 1.0 - 2048.0, A.mult, A.add)
+    ts(R("kcol"), R("ones", 0, 8), R("pf"), None, A.mult)
+    ts(R("omi"), R("row"), R("pf"), None, A.not_equal)
+    act(R("bo27"), R("bo"), F.Copy, None, 2.0 ** 27)
+    act(R("bo12"), R("bo"), F.Copy, None, 4096.0)
+    act(R("boh"), R("bo"), F.Copy)
+    act(R("kc"), R("jtf"), F.Identity, None, 0.0, 2048.0 - 2.0 ** 24)
+    act(R("kr"), R("b1", 0, 192), F.Copy)
     for k in range(8):
-        ts(R("th2", k, 512, 8), R("b1", 192, 256), 4096.0, -(2.0 ** 24), A.mult, A.add)
+        act(R("th2", k, 512, 8), R("b1", 192, 256), F.Identity, None, 4096.0, -(2.0 ** 24))
+    act(R("b1", 256, 512), R("pl"), F.Identity, None, None, R("pm"))
+    act(R("b1", 0, 256), R("pl"), F.Identity, None, 4095.0, R("pm4"))
+    fill(R("wb"), 0.0)
 
     def later_constants():
-        fill(R("ones"), 1.0)
-        ts(R("il"), R("i16"), R("pm"), None, A.add)
-        ts(R("pgc"), R("i1"), R("pg"), None, A.is_equal)
-        ts(R("eq0"), R("il"), 0.0, None, A.is_equal)
-        tt(R("tgt"), R("il"), R("eq0"), A.subtract)
-        ts(R("tc"), R("tgt"), -(2.0 ** 27), 2.0 ** 23 + 2048.0, A.mult, A.add)
-        ts(R("gc"), R("i16"), R("pf"), 128.0, A.is_equal, A.mult)
-        ts(R("pm16"), R("pm"), 16.0, None, A.add)
-        ts(R("self"), R("il"), 32.0, 4095.0 * 4096.0, A.mult, A.add)
-        ts(R("ioc"), R("il"), 32.0, 1.0 - 2048.0, A.mult, A.add)
         for k in range(8):
-            bank, c, w = SEG[k]
-            ts(R("ct", CTO[bank] + c, CTO[bank] + c + w), R("ones", 0, w), R("tc", k, k + 1), None, A.mult)
+            act(blk("grp", k), R("bo"), F.Copy, None, R("pgc", k, k + 1))
+        act(R("jt"), R("jtf"), F.Copy, None, 1.0 / 128.0)
+        act(R("ac"), R("row"), F.Identity, None, 32.0, 32.0)
         for k in range(8):
-            ts(blk("grp", k), R("bo"), R("pgc", k, k + 1), 1.0 if k < 4 else 0.5, A.mult, A.mult)
-            ts(blk("gsel", k), R("ones"), R("gc", k, k + 1), None, A.mult)
-        ts(R("omi"), R("row"), R("pf"), None, A.not_equal)
-        ts(R("bo27"), R("bo"), 2.0 ** 27, None, A.mult)
-        ts(R("bo12"), R("bo"), 4096.0, None, A.mult)
-        ts(R("boh"), R("bo"), 1.0, None, A.mult)
-        ts(R("kcol"), R("ones", 0, 8), R("pf"), None, A.mult)
-        ts(R("rst"), R("q16"), 0.0, None, A.is_gt)
-        ts(R("jt"), R("jtf"), 1.0 / 128.0, None, A.mult)
-        ts(R("ac"), R("row"), 32.0, 32.0, A.mult, A.add)
-        ts(R("b1", 256, 512), R("pl"), R("pm"), None, A.add)
-        ts(R("b1", 0, 256), R("b1", 256, 512), 1.0, 4095.0, A.add, A.mult)
+            act(blk("gsel", k), R("ones"), F.Copy, None, R("gc", k, k + 1))
     extra = []
 
     for t in range(3):
         X = "x%d" % t
         Xn = "x%d" % (t + 1)
         ko = "ko%d" % t
-        for s in range(16):
-            mm(R("b4", 0, 8), blk("ws", s), R(X, 32 * s + 31, 4096, 512), s == 0, s == 15)
+        mm(R("b4", 0, 128), R("bw"), R(X, 31, 4096, 32), True, True)
         for k in range(4):
             mm(blk("b5", k, 32), R("bw"), R(X, 32 * k + 31, 4096, 128), True, True)
         mm(R("b0"), R("idf"), R("kc"), True, False)
         act(R("xrep", 0, 128), R(X, 31, 4096, 32), F.Copy)
         for w in (128, 256, 512):
             act(R("xrep", w, 2 * w), R("xrep", 0, w), F.Copy)
-        cp(R("ui"), R("b4", 0, 8))
+        tt(R("mp"), R("b4", 0, 128), MK, A.mult)
+        scan(R("sp"), R("rst"), R("mp"), 0.0, A.mult, A.add)
+        cp(R("ui"), R("sp", 15, 128, 16))
         ts(R("ub"), R("ui"), 4095, None, A.bitwise_and)
         tt(R("sq"), R("ub"), R("ub"), A.mult)
         cp(R("uf"), R("ub"))
@@ -291,12 +288,12 @@ def rank_program(g, core, T, topo):
         def gather_s(k):
             m0, m1 = SCH[k]
             act(R("ga", 128 * m0, 128 * m1), R(X), F.Copy, R("cl", 8 * m0, 8 * m1))
-            for c in range(m0 // 4, m1 // 4):
+
+        def abs_s(k):
+            for c in range(SCH[k][0] // 4, SCH[k][1] // 4):
                 bank = R("b%d" % (6 + c % 2))
                 mm(bank, R("idb"), blk("ga", c, 512), True, False)
                 mm(bank, R("nid"), R("xrep", 0, 512), False, True)
-
-        def abs_s(k):
             for c in range(SCH[k][0] // 4, SCH[k][1] // 4):
                 act(blk("ab", c, 512), R("b%d" % (6 + c % 2)), F.Abs)
 
@@ -310,12 +307,11 @@ def rank_program(g, core, T, topo):
 
         e = 8 * LATE
         gather_s(0)
+        gather_s(1)
         for k, (m0, m1) in enumerate(VCH):
             tt(R("d", 128 * m0, 128 * m1), R(X), R("xrep", 0, 128 * (m1 - m0)), A.subtract, R("cl", 8 * m0, 8 * m1))
             if k < 2:
                 abs_s(k)
-                if k == 0:
-                    gather_s(1)
             act(R("ab", 128 * m0, 128 * m1), R("d", 128 * m0, 128 * m1), F.Abs)
             if k == 1:
                 ts(R("c16"), R("cl"), -2048.0, None, A.add)
@@ -325,15 +321,19 @@ def rank_program(g, core, T, topo):
                 dist(SCH[1][0], SCH[1][1], False)
                 mm(R("b7", 0, 512 - e), R("idf"), R("kc", e, 512), True, False)
                 mm(R("b7", 0, 512 - e), R("idh"), R("c16", e, 512), False, False)
-            if k >= 1:
-                dist(m0, m1, m1 == LATE or m1 == 64)
+            if 1 <= k and m1 <= LATE:
+                dist(m0, m1, m1 == LATE)
+        dist(LATE, 64, True)
         if t == 0:
-            later_constants()
+            for j in range(8):
+                bank, c, w = SEG[j]
+                act(R("ct", CTO[bank] + c, CTO[bank] + c + w), R("ones", 0, w), F.Copy, None, R("tc", j, j + 1))
         for bank, js in BANKS:
             mm(R(bank, 0, BANKW[bank]), R("idf"), R("ct", CTO[bank], CTO[bank] + BANKW[bank]), True, False)
+        if t == 0:
+            later_constants()
         cp(R("hI"), R("b5", 0, 128))
         ts(R("h63"), R("hI"), 63, None, A.bitwise_and)
-        fill(R("wb"), 0.0)
         for bank, a, b in (("b0", 0, e), ("b7", e, 512)):
             tt(R("gd", a, b), R(bank, 0, b - a), R("th2", a, b), A.is_lt)
             tt(R("mk", a, b), R(bank, 0, b - a), R("gd", a, b), A.mult)
@@ -349,10 +349,11 @@ def rank_program(g, core, T, topo):
         tt(R("jv"), R("jI"), R("jm"), A.mult)
         tt(R("ej"), R("jv"), MK, A.mult, E8)
         tt(R("ed"), R("dio"), R("mk2"), A.mult, R("expl"))
+        seg = {j: R(SEG[j][0], SEG[j][1], SEG[j][1] + SEG[j][2]) for j in range(8)}
         for bank, js in BANKS:
-            seg = {j: R(bank, SEG[j][1], SEG[j][1] + SEG[j][2]) for j in js}
             for j in js:
                 mm(seg[j], R("bo27"), R("ej", 0, SEG[j][2]), False, False)
+        for bank, js in BANKS:
             for j in js:
                 mm(seg[j], R("bo12"), R("ed", 0, SEG[j][2]), False, False)
                 mm(seg[j], R("boh"), R("ed", 128, 128 + SEG[j][2]), False, j == js[-1])
@@ -360,7 +361,7 @@ def rank_program(g, core, T, topo):
         ts(blk("b0", 1), R("h63"), 1.0, R("pm16"), A.add, A.mult)
         for bank, js in BANKS:
             for j in js:
-                red(R("accf", j, j + 1), R(bank, SEG[j][1], SEG[j][1] + SEG[j][2]), A.min, True)
+                red(R("accf", j, j + 1), seg[j], A.min, True)
         tt(R("acc"), R("accf"), R("self"), A.min)
         ts(R("fI"), R("acc"), 5, 127, A.arith_shift_right, A.bitwise_and)
         ts(R("cI"), R("acc"), 31, None, A.bitwise_and)
@@ -379,23 +380,21 @@ def rank_program(g, core, T, topo):
             lambda: red(R("lc"), R("b4", 0, 128), A.add),
             lambda: ts(R("kl"), R("kperm"), R("lc"), None, A.mult),
             lambda: ts(R("sk"), R("kl"), 7, None, A.arith_shift_right),
-            lambda: tt(R("pp", 0, 256, 2), R("sk"), blk("b0", 0), A.add),
-            lambda: tt(R("pp", 1, 256, 2), R("sk"), blk("b0", 1), A.add),
-            lambda: None,
+            lambda: (tt(R("pp", 0, 256, 2), R("sk"), blk("b0", 0), A.add),
+                     tt(R("pp", 1, 256, 2), R("sk"), blk("b0", 1), A.add)),
         ]
-        for k in range(6):
-            fk = R("f%d" % k)
+        for k in range(4):
             fl = R("fl%d" % k)
-            tt(R("mm"), fk, MK, A.mult, fl)
-            act(R("f%d" % (k + 1)), fk, F.Copy, fl)
-            if k < 4:
-                act(blk("lb", k, 256), blk("b%d" % (6 + k // 2), k % 2, 256), F.Copy)
+            act(R("h%d" % k), R("f%d" % k), F.Copy, fl)
             gaps[k]()
+            tt(R("mm"), R("h%d" % k), MK, A.mult, fl)
+            act(R("f%d" % (k + 1)), R("h%d" % k), F.Copy, fl)
+            act(blk("lb", k, 256), blk("b%d" % (6 + k // 2), k % 2, 256), F.Copy)
             scan(R("sc"), R("rst"), R("mm"), 0.0, A.mult, A.add)
             cp(R("fl%d" % (k + 1)), R("sc", 15, 128, 16))
         tt(R("b6", 0, 128), R("ac"), R("b4", 0, 128), A.subtract)
         mm(R("b4", 0, 8), R("idb"), R("kcol"), True, False)
-        act(R("f7"), R("f6"), F.Copy, R("fl6"))
+        act(R("f7"), R("f4"), F.Copy, R("fl4"))
         ts(R("b6", 256, 512), R("pp"), R("lc"), R("lc"), A.is_ge, A.mult)
         tt(R("pw"), R("pp"), R("b6", 256, 512), A.subtract)
         mm(R("b4", 0, 8), R("f7"), R("gsel", 0, 1024, 128), False, True)
@@ -414,10 +413,10 @@ def rank_program(g, core, T, topo):
             mm(R("b5", 0, 128), blk("lb", k), blk("cmp", k), False, k == 7)
         cp(R("plist"), R("pw"))
         tt(R("mp"), R("b5", 0, 128), MK, A.mult)
-        ts(R("t4"), R("b5", 0, 128), 4095.0, None, A.mult)
+        act(R("t4"), R("b5", 0, 128), F.Copy, None, 4095.0)
         scan(R("sp"), R("rst"), R("mp"), 0.0, A.mult, A.add)
-        tt(R("vrow"), R("t4"), R("b6", 0, 128), A.add)
         ts(R("cell"), R("sp", 15, 128, 16), 0.0625, -0.46875, A.mult, A.add)
+        tt(R("vrow"), R("t4"), R("b6", 0, 128), A.add)
         cp(R("celll"), R("cell"))
         cp(R("wb", 8, 264), R("vrow"), None, R("celll"))
         for a, b in ((0, LAYS), (LAYS, 256)):
@@ -431,26 +430,39 @@ def rank_program(g, core, T, topo):
                 cp(R("lay", 16 * a, 4096), R(X), R("sl", a, b))
             else:
                 act(R("lay", 0, 16 * b), R(X), F.Copy, R("sl", a, b))
-        o = MB * rank
-        for q, kr, a, b in (("V", 1, 0, 64), ("S", 3, 0, 64), ("V", 2, 0, 32), ("S", 2, 32, 64),
-                            ("V", 0, 0, 32), ("S", 0, 32, 64)):
-            to = R(Xn, o + 16 * a, o + 16 * b)
-            out = R(ko, MB * (kr - 1) + 16 * a, MB * (kr - 1) + 16 * b) if kr else to
+        to = blk(Xn, rank, MB)
+        ne = len(topo.engines(core, T.cores[(rank + 1) % N]))
+
+        def kids(q, kr, a, b):
+            buf, o = (ko, MB * (kr - 1)) if kr else (Xn, MB * rank)
             lst = R("plist", 64 * kr + a, 64 * kr + b)
             if q == "V":
-                cp(out, R("lay"), lst)
+                cp(R(buf, o + 16 * a, o + 16 * b), R("lay"), lst)
             else:
-                act(out, R("lay"), F.Copy, lst)
-            if kr:
+                act(R(buf, o + 16 * a, o + 16 * b), R("lay"), F.Copy, lst)
+
+        def send(krs):
+            tr = []
+            for n, kr in enumerate(krs):
                 dst = T.cores[(kr + rank) % N]
                 rid, pid, _ = topo.addr(dst)
-                sync("G", [], [out])
-                g.remote_dma(out_ap=ap(to), in_ap=ap(out), remote_sem=T.sem["ar%d_%d" % (t, kr)],
-                             local_sem=T.sem["ls%d" % t], pid=pid, routing_id=rid, dma_engine_mask=topo.mask(core, dst))
-        ne = len(topo.engines(core, T.cores[(rank + 1) % N]))
-        extra.append(("ls%d" % t, 4 * ne))
+                mask = sum(1 << x for x in topo.engines(core, dst)[n::len(krs)])
+                tr.append(RemoteDMATransfer(dst_ids=[DstId(rid=rid, pnc=pid)], dma_engine_mask=mask, dst=ap(to),
+                                            remote_sem=T.sem["ar%d_%d" % (t, kr)], src=ap(blk(ko, kr - 1, MB))))
+            sync("G", [], [blk(ko, kr - 1, MB) for kr in krs])
+            g.remote_dma_fused(tr, local_sem=T.sem["ls%d" % t])
+        kids("V", 1, 0, 64)
+        kids("S", 3, 0, 64)
+        send((1, 3))
+        kids("V", 2, 0, 32)
+        kids("S", 2, 32, 64)
+        send((2,))
+        kids("V", 0, 0, 32)
+        kids("S", 0, 32, 64)
+        fill(R("wb"), 0.0)
+        extra.append(("ls%d" % t, 2 * ne))
         for kr in (1, 2, 3):
-            arrive("ar%d_%d" % (t, kr), ne * (2 if kr == 2 else 1), [blk(Xn, (rank - kr) % N, MB)])
+            arrive("ar%d_%d" % (t, kr), ne if kr == 2 else ne // 2, [blk(Xn, (rank - kr) % N, MB)])
     for kr in (0, 1, 3, 2):
         s = (rank - kr) % N
         dma("Y", T.y[:, MB * s:MB * s + MB], T.x3[:, MB * s:MB * s + MB], [], [blk("x3", s, MB)])

@@ -14,24 +14,25 @@ for _bank, _js in BANKS:
         _c += 16 * (_j + 1)
 BANKW = {"b2": 240, "b3": 176, "b4": 160}
 CTO = {"b2": 0, "b3": 240, "b4": 416}
-SCH = [(0, 8), (8, 12)]
-VCH = [(12, 20), (20, 28), (28, 36), (36, 44), (44, 52), (52, 58), (58, 62), (62, 64)]
-LATE = 58
-LAYS = 148
+SCH = [(0, 8), (8, 16)]
+VCH = [(16, 24), (24, 32), (32, 40), (40, 48), (48, 56), (56, 60), (60, 64)]
+LATE = 56
+LAYS = 136
 
 _f, _h, _b, _i, _u = "float32", "float16", "bfloat16", "int32", "uint16"
 _sb = {
-    _b: "x0:4096 x1:4096 x2:4096 x3:4096 lay:4096 ko0:3072 ko1:3072 ko2:3072 q16:128 q17:128 bq:128 bo:128 bo27:128 "
-        "mk2:256 idb:128 nid:128 ld:2048 bw:128 ones:128 omi:128 gsel:1024 grp:1024 jt:512 kcol:8 rst:128 "
-        "xrep:1024 ga:2048 d:8192 ab:8192 gd:512 ej:128 ef:128 el:128 mm:128 lb:1024 cmp:1024 "
+    _b: "x0:4096 x1:4096 x2:4096 x3:4096 lay:4096 ko0:3072 ko1:3072 ko2:3072 lr0:512 lr1:512 q16:128 q17:128 bq:128 "
+        "bo:128 bo27:128 mk2:256 idb:128 nid:128 ld:2048 bw:128 ones:128 omi:128 gsel:1024 grp:1024 jt:512 kcol:8 "
+        "rst:128 xrep:1024 ga:2048 d:8192 ab:8192 gd:512 ej:128 ef:128 el:128 mm:128 lb:1024 cmp:1024 "
         "f0:128 f1:128 f2:128 f3:128 f4:128 f7:128 h0:128 h1:128 h2:128 h3:128",
     _h: "bo12:128 boh:128 idh:128 c16:512 ed:256",
     _f: "wtf:1 ekt:256 kr:192 th2:512 pf:1 pm:1 pm16:1 pm4:1 pg:1 row:128 mg:128 bof:128 idf:128 i16:8 i1:8 gc:8 "
         "pgc:8 negr:8 jtf:512 kc:512 il:8 eq0:8 tgt:8 tc:8 ct:576 self:8 ioc:8 pl:256 kperm:128 ac:128 uf:8 u2:8 "
-        "mk:512 bf:8 jm:8 accf:8 sc:128 lc:1 pp:256 pw:256 mp:128 t4:128 vrow:128 sp:128 wb:264 w1:256 ff:256",
-    _i: "wti:1 kt:16 pi:1 pmi:1 pgi:1 expi:16 ui:8 ub:8 sq:8 s5:8 cv:512 ci:512 best:8 jI:8 dI:8 oI:8 jv:8 dio:16 "
-        "acc:8 fI:8 cI:8 lI:8 hI:128 h63:128 kl:128 sk:128 cell:8 si:256 sj:256",
-    _u: "expl:16 cl:512 plist:256 celll:8 sl:256 fl0:8 fl1:8 fl2:8 fl3:8 fl4:8",
+        "h31:8 w31:8 q31:8 mk:512 bf:8 jm:8 accf:8 sc:128 lc:1 pp:256 pw:256 mp:128 t4:128 vrow:128 sp:128 wb:264 "
+        "w1:256 ff:256",
+    _i: "wti:1 kt:16 pi:1 pmi:1 pgi:1 expi:16 ui:8 ub:8 sq:8 s5:8 cv:512 ci:512 best:8 jI:8 oI:8 jv:8 dio:16 "
+        "acc:8 fI:8 cI:8 lI:8 hI:128 h63:128 kl:128 sk:128 hb:8 k31:8 s31:8 p31:8 cell:8 si:256 sj:256",
+    _u: "expl:16 cl:512 plist:256 celll:8 l31:8 sl:256 fl0:8 fl1:8 fl2:8 fl3:8 fl4:8",
 }
 WIDTH, TYPE, PLACE, SCRATCH, _used = {}, {}, {}, {}, {}
 for _t, _list in _sb.items():
@@ -49,7 +50,7 @@ for _k in range(8):
     SCRATCH["b%d" % _k] = ("psum", [128, 512], _f)
     WIDTH["b%d" % _k], TYPE["b%d" % _k], PLACE["b%d" % _k] = 512, _f, ("b%d" % _k, 0)
 SEMAPHORES = ["qV", "qS", "qP", "qG"] + ["dl%d" % k for k in range(12)] + \
-    ["ar%d_%d" % (t, k) for t in range(3) for k in range(4)] + ["ls%d" % t for t in range(3)]
+    ["ar%d_%d" % (t, k) for t in range(3) for k in range(4)] + ["%s%d" % (s, t) for t in range(3) for s in ("ls", "lq", "sm")]
 
 
 def build_tracker(g, T):
@@ -249,7 +250,6 @@ def rank_program(g, core, T, topo):
         act(R("th2", k, 512, 8), R("b1", 192, 256), F.Identity, None, 4096.0, -(2.0 ** 24))
     act(R("b1", 256, 512), R("pl"), F.Identity, None, None, R("pm"))
     act(R("b1", 0, 256), R("pl"), F.Identity, None, 4095.0, R("pm4"))
-    fill(R("wb"), 0.0)
 
     def later_constants():
         for k in range(8):
@@ -259,18 +259,27 @@ def rank_program(g, core, T, topo):
         for k in range(8):
             act(blk("gsel", k), R("ones"), F.Copy, None, R("gc", k, k + 1))
     extra = []
+    ne = len(topo.engines(core, T.cores[(rank + 1) % N]))
+    far = [kr for kr in (1, 2, 3) if topo.die(T.cores[(kr + rank) % N]) != topo.die(core)]
+    near = [kr for kr in (1, 2, 3) if kr not in far]
 
     for t in range(3):
         X = "x%d" % t
         Xn = "x%d" % (t + 1)
         ko = "ko%d" % t
-        mm(R("b4", 0, 128), R("bw"), R(X, 31, 4096, 32), True, True)
+        for r in range(N):
+            if t:
+                last = R("lr%d" % (t - 1), 128 * r + (rank - r) % N, 128 * r + 128, 4)
+            else:
+                last = R(X, MB * r + 31, MB * r + MB, 32)
+            mm(blk("b4", r, 32), R("bw"), last, True, True)
+            act(blk("xrep", r, 32), last, F.Copy)
+        mm(R("b0"), R("idf"), R("kc"), True, False)
         for k in range(4):
             mm(blk("b5", k, 32), R("bw"), R(X, 32 * k + 31, 4096, 128), True, True)
-        mm(R("b0"), R("idf"), R("kc"), True, False)
-        act(R("xrep", 0, 128), R(X, 31, 4096, 32), F.Copy)
         for w in (128, 256, 512):
             act(R("xrep", w, 2 * w), R("xrep", 0, w), F.Copy)
+        act(R("wb"), R("jtf", 0, 264), F.Copy, None, 0.0)
         tt(R("mp"), R("b4", 0, 128), MK, A.mult)
         scan(R("sp"), R("rst"), R("mp"), 0.0, A.mult, A.add)
         cp(R("ui"), R("sp", 15, 128, 16))
@@ -281,9 +290,10 @@ def rank_program(g, core, T, topo):
         cp(R("u2"), R("s5"))
         for k in range(8):
             ts(R("cv", k, 512, 8), blk("kr", t, 64), R("uf", k, k + 1), R("u2", k, k + 1), A.mult, A.add)
-        for a, b in ((0, 160), (160, 512)):
+        for a, b in ((0, 128), (128, 512)):
             ts(R("ci", a, b), R("cv", a, b), 4095, None, A.bitwise_and)
             cp(R("cl", a, b), R("ci", a, b))
+        ts(R("c16"), R("cl"), -2048.0, None, A.add)
 
         def gather_s(k):
             m0, m1 = SCH[k]
@@ -314,7 +324,6 @@ def rank_program(g, core, T, topo):
                 abs_s(k)
             act(R("ab", 128 * m0, 128 * m1), R("d", 128 * m0, 128 * m1), F.Abs)
             if k == 1:
-                ts(R("c16"), R("cl"), -2048.0, None, A.add)
                 mm(R("b0"), R("idh"), R("c16"), False, False)
                 dist(SCH[0][0], SCH[0][1], False)
                 dist(VCH[0][0], VCH[0][1], False)
@@ -334,17 +343,18 @@ def rank_program(g, core, T, topo):
             later_constants()
         cp(R("hI"), R("b5", 0, 128))
         ts(R("h63"), R("hI"), 63, None, A.bitwise_and)
+        ts(R("hb"), R("ub"), 63, None, A.bitwise_and)
+        ts(R("h31"), R("hb"), 1.0, 31.0, A.add, A.mult)
         for bank, a, b in (("b0", 0, e), ("b7", e, 512)):
             tt(R("gd", a, b), R(bank, 0, b - a), R("th2", a, b), A.is_lt)
             tt(R("mk", a, b), R(bank, 0, b - a), R("gd", a, b), A.mult)
         for k in range(8):
             red(R("bf", k, k + 1), R("mk", k, 512, 8), A.min)
+        ts(R("dio", 0, 8), R("bf"), 2.0 ** -12, 2047.5 + 2.0 ** -13, A.mult, A.add)
         cp(R("best"), R("bf"))
         ts(R("jI"), R("best"), 5, 127, A.arith_shift_right, A.bitwise_and)
-        ts(R("dI"), R("best"), 12, None, A.arith_shift_right)
         ts(R("oI"), R("best"), 1, 15, A.arith_shift_right, A.bitwise_and)
         tt(R("jm"), R("jI"), R("il"), A.is_gt)
-        ts(R("dio", 0, 8), R("dI"), 2048.0, None, A.add)
         tt(R("dio", 8, 16), R("oI"), R("ioc"), A.add)
         tt(R("jv"), R("jI"), R("jm"), A.mult)
         tt(R("ej"), R("jv"), MK, A.mult, E8)
@@ -378,8 +388,9 @@ def rank_program(g, core, T, topo):
         mm(R("b3"), blk("gsel", 0), R("jt"), True, False)
         gaps = [
             lambda: red(R("lc"), R("b4", 0, 128), A.add),
-            lambda: ts(R("kl"), R("kperm"), R("lc"), None, A.mult),
-            lambda: ts(R("sk"), R("kl"), 7, None, A.arith_shift_right),
+            lambda: (ts(R("kl"), R("kperm"), R("lc"), None, A.mult), ts(R("k31"), R("il"), R("lc"), None, A.mult)),
+            lambda: (ts(R("sk"), R("kl"), 7, None, A.arith_shift_right),
+                     ts(R("s31"), R("k31"), 7, None, A.arith_shift_right)),
             lambda: (tt(R("pp", 0, 256, 2), R("sk"), blk("b0", 0), A.add),
                      tt(R("pp", 1, 256, 2), R("sk"), blk("b0", 1), A.add)),
         ]
@@ -396,7 +407,9 @@ def rank_program(g, core, T, topo):
         mm(R("b4", 0, 8), R("idb"), R("kcol"), True, False)
         act(R("f7"), R("f4"), F.Copy, R("fl4"))
         ts(R("b6", 256, 512), R("pp"), R("lc"), R("lc"), A.is_ge, A.mult)
+        tt(R("p31"), R("s31"), R("h31"), A.add)
         tt(R("pw"), R("pp"), R("b6", 256, 512), A.subtract)
+        ts(R("w31"), R("p31"), R("lc"), R("lc"), A.is_ge, A.mult)
         mm(R("b4", 0, 8), R("f7"), R("gsel", 0, 1024, 128), False, True)
         act(R("negr", 4, 8), R("b4", 4, 8), F.Copy, None, -1.0)
         order = (4, 5, 6, 7, 0, 1, 2, 3)
@@ -411,7 +424,9 @@ def rank_program(g, core, T, topo):
                 act(blk("cmp", k), blk("b3", k % 4), F.Sign, None, None, R("negr", k, k + 1))
         for k in (0, 1, 4, 5, 2, 3, 6, 7):
             mm(R("b5", 0, 128), blk("lb", k), blk("cmp", k), False, k == 7)
+        tt(R("q31"), R("p31"), R("w31"), A.subtract)
         cp(R("plist"), R("pw"))
+        cp(R("l31"), R("q31"))
         tt(R("mp"), R("b5", 0, 128), MK, A.mult)
         act(R("t4"), R("b5", 0, 128), F.Copy, None, 4095.0)
         scan(R("sp"), R("rst"), R("mp"), 0.0, A.mult, A.add)
@@ -419,19 +434,28 @@ def rank_program(g, core, T, topo):
         tt(R("vrow"), R("t4"), R("b6", 0, 128), A.add)
         cp(R("celll"), R("cell"))
         cp(R("wb", 8, 264), R("vrow"), None, R("celll"))
-        for a, b in ((0, LAYS), (LAYS, 256)):
-            tt(R("b7", a, b), R("wb", 8 + a, 8 + b), R("b1", a, b), A.is_lt)
-            tt(R("w1", a, b), R("wb", 8 + a, 8 + b), R("b7", a, b), A.mult)
-            scan(R("ff", a, b), R("wb", 7 + a, 7 + b), R("w1", a, b), R("ff", a - 1, a) if a else 0.0, A.max, A.max)
-            tt(R("si", a, b), R("ff", a, b), R("b1", 256 + a, 256 + b), A.add)
-            ts(R("sj", a, b), R("si", a, b), 4095, None, A.bitwise_and)
-            cp(R("sl", a, b), R("sj", a, b))
-            if a:
-                cp(R("lay", 16 * a, 4096), R(X), R("sl", a, b))
+
+        def step(n, a, b):
+            if n == 0:
+                tt(R("b7", a, b), R("wb", 8 + a, 8 + b), R("b1", a, b), A.is_lt)
+            elif n == 1:
+                tt(R("w1", a, b), R("wb", 8 + a, 8 + b), R("b7", a, b), A.mult)
+            elif n == 2:
+                scan(R("ff", a, b), R("wb", 7 + a, 7 + b), R("w1", a, b), R("ff", a - 1, a) if a else 0.0, A.max, A.max)
+            elif n == 3:
+                tt(R("si", a, b), R("ff", a, b), R("b1", 256 + a, 256 + b), A.add)
+            elif n == 4:
+                ts(R("sj", a, b), R("si", a, b), 4095, None, A.bitwise_and)
             else:
-                act(R("lay", 0, 16 * b), R(X), F.Copy, R("sl", a, b))
+                cp(R("sl", a, b), R("sj", a, b))
+        for n, second in ((0, 0), (0, 1), (1, 0), (1, 1), (2, 0), (3, 0), (2, 1), (4, 0), (3, 1), (5, 0), (4, 1), (5, 1)):
+            if second:
+                step(n, LAYS, 256)
+            else:
+                step(n, 0, LAYS)
+        act(R("lay", 0, 16 * LAYS), R(X), F.Copy, R("sl", 0, LAYS))
+        cp(R("lay", 16 * LAYS, 4096), R(X), R("sl", LAYS, 256))
         to = blk(Xn, rank, MB)
-        ne = len(topo.engines(core, T.cores[(rank + 1) % N]))
 
         def kids(q, kr, a, b):
             buf, o = (ko, MB * (kr - 1)) if kr else (Xn, MB * rank)
@@ -441,29 +465,28 @@ def rank_program(g, core, T, topo):
             else:
                 act(R(buf, o + 16 * a, o + 16 * b), R("lay"), F.Copy, lst)
 
-        def send(krs):
-            tr = []
-            for n, kr in enumerate(krs):
-                dst = T.cores[(kr + rank) % N]
-                rid, pid, _ = topo.addr(dst)
-                mask = sum(1 << x for x in topo.engines(core, dst)[n::len(krs)])
-                tr.append(RemoteDMATransfer(dst_ids=[DstId(rid=rid, pnc=pid)], dma_engine_mask=mask, dst=ap(to),
-                                            remote_sem=T.sem["ar%d_%d" % (t, kr)], src=ap(blk(ko, kr - 1, MB))))
-            sync("G", [], [blk(ko, kr - 1, MB) for kr in krs])
-            g.remote_dma_fused(tr, local_sem=T.sem["ls%d" % t])
-        kids("V", 1, 0, 64)
-        kids("S", 3, 0, 64)
-        send((1, 3))
-        kids("V", 2, 0, 32)
-        kids("S", 2, 32, 64)
-        send((2,))
-        kids("V", 0, 0, 32)
-        kids("S", 0, 32, 64)
-        fill(R("wb"), 0.0)
-        extra.append(("ls%d" % t, 2 * ne))
+        def send(krs, buf, into, rs, ls):
+            dsts = [T.cores[(kr + rank) % N] for kr in krs]
+            ids = [DstId(rid=topo.addr(dst)[0], pnc=topo.addr(dst)[1]) for dst in dsts]
+            sync("G", [], [buf])
+            g.remote_dma_fused([RemoteDMATransfer(dst_ids=ids, dma_engine_mask=topo.mask(core, dsts[0]), srcs=[ap(buf)],
+                                                  dsts=[ap(into) for _ in krs], remote_sem=T.sem[rs])],
+                               local_sem=T.sem[ls])
+        if t < 2:
+            lr = "lr%d" % t
+            cp(blk(lr, rank), R("lay"), R("l31"))
+            send((1, 2, 3), blk(lr, rank), blk(lr, rank), "sm%d" % t, "lq%d" % t)
+            arrive("sm%d" % t, 3 * ne, [blk(lr, r) for r in range(N) if r != rank])
+            extra.append(("lq%d" % t, ne))
+        for kr in far + near + [0]:
+            kids("V", kr, 0, 32)
+            kids("S", kr, 32, 64)
+            if kr:
+                send((kr,), blk(ko, kr - 1, MB), to, "ar%d_%d" % (t, kr), "ls%d" % t)
+        extra.append(("ls%d" % t, 3 * ne))
         for kr in (1, 2, 3):
-            arrive("ar%d_%d" % (t, kr), ne if kr == 2 else ne // 2, [blk(Xn, (rank - kr) % N, MB)])
-    for kr in (0, 1, 3, 2):
+            arrive("ar%d_%d" % (t, kr), ne, [blk(Xn, (rank - kr) % N, MB)])
+    for kr in [0] + [(-k) % N for k in far + near]:
         s = (rank - kr) % N
         dma("Y", T.y[:, MB * s:MB * s + MB], T.x3[:, MB * s:MB * s + MB], [], [blk("x3", s, MB)])
     finish(extra)

from concourse.bass import DstId, RemoteDMATransfer
from concourse.mybir import AluOpType, AxisListType, ActivationFunctionType

A = AluOpType
F = ActivationFunctionType
N = 4
MB = 1024
BANKS = (("b2", (7, 6)), ("b3", (5, 4)), ("b4", (3, 2, 1, 0)))
SEG = {}
for _bank, _js in BANKS:
    _c = 0
    for _j in _js:
        SEG[_j] = (_bank, _c, 16 * (_j + 1))
        _c += 16 * (_j + 1)
BANKW = {"b2": 240, "b3": 176, "b4": 160}
CTO = {"b2": 0, "b3": 240, "b4": 416}
SCH = [(0, 8), (8, 16)]
VCH = [(16, 24), (24, 32), (32, 40), (40, 48), (48, 56), (56, 60), (60, 64)]
LATE = 56
LAYS = 136

_f, _h, _b, _i, _u = "float32", "float16", "bfloat16", "int32", "uint16"
_sb = {
    _b: "x0:4096 x1:4096 x2:4096 x3:4096 lay:4096 ko0:3072 ko1:3072 ko2:3072 lr0:512 lr1:512 q16:128 q17:128 bq:128 "
        "bo:128 bo27:128 mk2:256 idb:128 nid:128 ld:2048 bw:128 ones:128 omi:128 gsel:1024 grp:1024 jt:512 kcol:8 "
        "rst:128 xrep:1024 ga:2048 d:8192 ab:8192 gd:512 ej:128 ef:128 el:128 mm:128 lb:1024 cmp:1024 "
        "f0:128 f1:128 f2:128 f3:128 f4:128 f7:128 h0:128 h1:128 h2:128 h3:128",
    _h: "bo12:128 boh:128 idh:128 c16:512 ed:256",
    _f: "wtf:1 ekt:256 kr:192 th2:512 pf:1 pm:1 pm16:1 pm4:1 pg:1 row:128 mg:128 bof:128 idf:128 i16:8 i1:8 gc:8 "
        "pgc:8 negr:8 jtf:512 kc:512 il:8 eq0:8 tgt:8 tc:8 ct:576 self:8 ioc:8 pl:256 kperm:128 ac:128 uf:8 u2:8 "
        "h31:8 w31:8 q31:8 mk:512 bf:8 jm:8 accf:8 sc:128 lc:1 pp:256 pw:256 mp:128 t4:128 vrow:128 sp:128 wb:264 "
        "w1:256 ff:256",
    _i: "wti:1 kt:16 pi:1 pmi:1 pgi:1 expi:16 ui:8 ub:8 sq:8 s5:8 cv:512 ci:512 best:8 jI:8 oI:8 jv:8 dio:16 "
        "acc:8 fI:8 cI:8 lI:8 hI:128 h63:128 kl:128 sk:128 hb:8 k31:8 s31:8 p31:8 cell:8 si:256 sj:256",
    _u: "expl:16 cl:512 plist:256 celll:8 l31:8 sl:256 fl0:8 fl1:8 fl2:8 fl3:8 fl4:8",
}
WIDTH, TYPE, PLACE, SCRATCH, _used = {}, {}, {}, {}, {}
for _t, _list in _sb.items():
    for _e in _list.split():
        _k, _w = _e.split(":")
        WIDTH[_k], TYPE[_k], PLACE[_k] = int(_w), _t, (_k, 0)
        if int(_w) <= 16 and _k not in ("wti", "kt"):
            PLACE[_k] = ("small_" + _t, _used.get(_t, 0))
            _used[_t] = _used.get(_t, 0) + 16
        else:
            SCRATCH[_k] = ("sbuf", [128, int(_w)], _t)
for _k, _v in _used.items():
    SCRATCH["small_" + _k] = ("sbuf", [128, _v], _k)
for _k in range(8):
    SCRATCH["b%d" % _k] = ("psum", [128, 512], _f)
    WIDTH["b%d" % _k], TYPE["b%d" % _k], PLACE["b%d" % _k] = 512, _f, ("b%d" % _k, 0)
SEMAPHORES = ["qV", "qS", "qP", "qG"] + ["dl%d" % k for k in range(12)] + \
    ["ar%d_%d" % (t, k) for t in range(3) for k in range(4)] + ["%s%d" % (s, t) for t in range(3) for s in ("ls", "lq", "sm")]


def build_tracker(g, T):
    eng = {"V": g.vector, "S": g.scalar, "P": g.tensor, "G": g, "Y": g.sync}
    cnt = {"V": 0, "S": 0, "P": 0, "G": 0}
    clk = {q: {} for q in eng}
    snap = {}
    acc = {}
    ndma = [0]

    def meet(r, e):
        if r[1] >= e[3] or e[2] >= r[2]:
            return False
        return not (r[3] == e[4] and r[3] > 1 and (r[1] - e[2]) % r[3])

    def sync(q, outs, ins):
        need = {}
        for w, regs in ((True, outs), (False, ins)):
            for r in regs:
                psum = SCRATCH[r[0]][0] == "psum"
                for e in acc.get(r[0], ()):
                    hit = (psum and e[0] != q) or ((w or e[5]) and (q, e[0]) != ("P", "P") and meet(r, e))
                    tok = e[1]
                    if hit and clk[q].get(tok[0], 0) < tok[1] and need.get(tok[0], 0) < tok[1]:
                        need[tok[0]] = tok[1]
        items = sorted(need.items(), key=lambda kv: kv[0])
        for s, v in items:
            if not any(s2 != s and snap[(s2, v2)].get(s, 0) >= v for s2, v2 in items):
                eng[q].wait_ge(T.sem[s], v)
        for tok in items:
            for s, v in snap[tok].items():
                clk[q][s] = max(v, clk[q].get(s, 0))

    def note(q, tok, outs, ins):
        for w, regs in ((True, outs), (False, ins)):
            for r in regs:
                lst = acc.setdefault(r[0], [])
                lst[:] = [e for e in lst if not (e[0] == q and (e[5] == w or w) and e[2] >= r[1] and e[3] <= r[2]
                                                 and (r[3] == 1 or (e[4] == r[3] and (e[2] - r[1]) % r[3] == 0)))]
                lst.append((q, tok, r[1], r[2], r[3], w))

    def done(q, who, tok, outs, ins):
        snap[tok] = dict(clk[q]) if q else {}
        snap[tok][tok[0]] = tok[1]
        note(who, tok, outs, ins)

    def emit(q, call, outs, ins):
        sync(q, outs, ins)
        cnt[q] += 1
        call(eng[q]).then_inc(T.sem["q" + q], 1)
        done(q, q, ("q" + q, cnt[q]), outs, ins)

    def dma(q, out_ap, in_ap, outs, ins):
        sync(q, outs, ins)
        s = "dl%d" % ndma[0]
        ndma[0] += 1
        eng[q].dma_start(out_ap, in_ap).then_inc(T.sem[s], 16)
        done(q, s, (s, 16), outs, ins)

    def arrive(s, val, outs):
        done(None, s, (s, val), outs, ())

    def finish(extra):
        for q in ("V", "S", "P", "G"):
            g.wait_ge(T.sem["q" + q], cnt[q])
        for k in range(ndma[0]):
            g.wait_ge(T.sem["dl%d" % k], 16)
        for s, v in extra:
            g.wait_ge(T.sem[s], v)
    return emit, dma, sync, arrive, finish


def rank_program(g, core, T, topo):
    rank = T.rank_of(core)
    if rank is None:
        return
    emit, dma, sync, arrive, finish = build_tracker(g, T)

    def R(name, a=0, b=None, st=1):
        p, o = PLACE[name]
        return (p, o + a, o + (WIDTH[name] if b is None else b), st)

    def blk(name, k, w=128):
        return R(name, w * k, w * k + w)

    def ap(r):
        if r[3] == 1:
            return T[r[0]][:, r[1]:r[2]]
        return T[r[0]][:, r[1]:r[2]:r[3]]

    def src(r, idx):
        return ap(r) if idx is None else ap(r).indirect(ap(idx))

    def regs(*rs):
        return [r for r in rs if isinstance(r, tuple)]

    def sca(v):
        return ap(v) if isinstance(v, tuple) else v

    def tt(out, in0, in1, op, idx=None):
        emit("V", lambda e: e.tensor_tensor(ap(out), src(in0, idx), ap(in1), op), [out], regs(in0, in1, idx))

    def ts(out, in0, s1, s2, op0, op1=None):
        if op1 is None:
            emit("V", lambda e: e.tensor_scalar(ap(out), ap(in0), sca(s1), None, op0), [out], regs(in0, s1))
        else:
            emit("V", lambda e: e.tensor_scalar(ap(out), ap(in0), sca(s1), sca(s2), op0, op1), [out], regs(in0, s1, s2))

    def cp(out, in_, idx=None, oidx=None):
        emit("V", lambda e: e.tensor_copy(src(out, oidx), src(in_, idx)), [out], regs(in_, idx, oidx))

    def fill(out, v):
        emit("V", lambda e: e.memset(ap(out), v), [out], [])

    def red(out, in_, op, absv=False):
        emit("V", lambda e: e.tensor_reduce(ap(out), ap(in_), AxisListType.X, op, apply_absolute_value=absv), [out], [in_])

    def scan(out, d0, d1, init, op0, op1):
        emit("V", lambda e: e.tensor_tensor_scan(ap(out), ap(d0), ap(d1), sca(init), op0, op1), [out], regs(d0, d1, init))

    def act(out, in_, fn, idx=None, scale=None, bias=None):
        kw = {}
        if scale is not None:
            kw["scale"] = sca(scale)
        if bias is not None:
            kw["bias"] = sca(bias)
        emit("S", lambda e: e.activation(ap(out), src(in_, idx), fn, **kw), [out], regs(in_, idx, scale, bias))

    def mm(out, lhsT, rhs, start, stop):
        emit("P", lambda e: e.matmul(ap(out), ap(lhsT), ap(rhs), start, stop), [out], [lhsT, rhs])

    def iota(name, pattern, cm=0):
        out = R(name)
        kw = {} if TYPE[name] == _i else {"allow_small_or_imprecise_dtypes": True}
        emit("G", lambda e: e.iota(ap(out), pattern, 0, cm, **kw), [out], [])

    dma("Y", T.x0[:], T.gen0[:], [R("x0")], [])
    dma("S", T.kt[:, 0:12], T.km[:], [R("kt", 0, 12)], [])
    dma("S", T.kt[:, 12:16], T.th[:], [R("kt", 12, 16)], [])
    dma("S", T.wti[:], T.wt[:], [R("wti")], [])

    iota("pi", [[0, 1]], 1)
    iota("q16", [[0, 8], [1, 16]])
    iota("mg", [[1, 8], [0, 16]])
    iota("expi", [[1, 16]])
    iota("row", [[1, 128]])
    iota("i16", [[16, 8]])
    iota("i1", [[1, 8]])
    iota("kperm", [[1, 4], [4, 32]])
    iota("jtf", [[0, 4], [1, 128]])
    iota("pl", [[16, 256]])
    MK = R("mk2", 0, 128)
    E8 = R("expl", 0, 8)
    cp(R("pf"), R("pi"))
    ts(R("pmi"), R("pi"), 15, None, A.bitwise_and)
    ts(R("pgi"), R("pi"), 4, None, A.arith_shift_right)
    cp(R("expl"), R("expi"))
    cp(R("pm"), R("pmi"))
    cp(R("pg"), R("pgi"))
    ts(R("q17"), R("q16"), 1.0, None, A.add)
    ts(R("bo"), R("mg"), R("pg"), None, A.is_equal)
    ts(R("bof"), R("mg"), R("pg"), None, A.is_equal)
    ts(MK, R("q16"), R("pm"), None, A.is_equal)
    ts(R("mk2", 128, 256), R("q16"), R("pm"), None, A.is_equal)
    tt(R("bq"), R("q17"), R("bo"), A.mult)
    for s in range(16):
        ts(blk("ld", s), R("bq"), float(s + 1), 4096.0, A.is_equal, A.mult)
    cp(R("wtf"), R("wti"))
    ts(R("bw"), R("bo"), R("wtf"), None, A.mult)
    tt(R("ekt"), R("kt"), R("mk2"), A.mult, R("expl"))
    mm(R("b1", 0, 256), R("bof"), R("ekt"), True, True)
    ts(R("idf"), R("row"), R("pf"), None, A.is_equal)
    ts(R("idb"), R("row"), R("pf"), None, A.is_equal)
    ts(R("nid"), R("row"), R("pf"), -1.0, A.is_equal, A.mult)
    ts(R("idh"), R("row"), R("pf"), None, A.is_equal)
    ts(R("rst"), R("q16"), 0.0, None, A.is_gt)
    fill(R("ones"), 1.0)
    ts(R("il"), R("i16"), R("pm"), None, A.add)
    ts(R("pgc"), R("i1"), R("pg"), None, A.is_equal)
    ts(R("gc"), R("i16"), R("pf"), 128.0, A.is_equal, A.mult)
    ts(R("eq0"), R("il"), 0.0, None, A.is_equal)
    ts(R("pm16"), R("pm"), 16.0, None, A.add)
    ts(R("pm4"), R("pm"), 4095.0, 4095.0, A.mult, A.add)
    tt(R("tgt"), R("il"), R("eq0"), A.subtract)
    ts(R("pgc", 4, 8), R("pgc", 4, 8), 0.5, None, A.mult)
    ts(R("self"), R("il"), 32.0, 4095.0 * 4096.0, A.mult, A.add)
    ts(R("tc"), R("tgt"), -(2.0 ** 27), 2.0 ** 23 + 2048.0, A.mult, A.add)
    ts(R("ioc"), R("il"), 32.0, 1.0 - 2048.0, A.mult, A.add)
    ts(R("kcol"), R("ones", 0, 8), R("pf"), None, A.mult)
    ts(R("omi"), R("row"), R("pf"), None, A.not_equal)
    act(R("bo27"), R("bo"), F.Copy, None, 2.0 ** 27)
    act(R("bo12"), R("bo"), F.Copy, None, 4096.0)
    act(R("boh"), R("bo"), F.Copy)
    act(R("kc"), R("jtf"), F.Identity, None, 0.0, 2048.0 - 2.0 ** 24)
    act(R("kr"), R("b1", 0, 192), F.Copy)
    for k in range(8):
        act(R("th2", k, 512, 8), R("b1", 192, 256), F.Identity, None, 4096.0, -(2.0 ** 24))
    act(R("b1", 256, 512), R("pl"), F.Identity, None, None, R("pm"))
    act(R("b1", 0, 256), R("pl"), F.Identity, None, 4095.0, R("pm4"))

    def later_constants():
        for k in range(8):
            act(blk("grp", k), R("bo"), F.Copy, None, R("pgc", k, k + 1))
        act(R("jt"), R("jtf"), F.Copy, None, 1.0 / 128.0)
        act(R("ac"), R("row"), F.Identity, None, 32.0, 32.0)
        for k in range(8):
            act(blk("gsel", k), R("ones"), F.Copy, None, R("gc", k, k + 1))
    extra = []
    ne = len(topo.engines(core, T.cores[(rank + 1) % N]))
    far = [kr for kr in (1, 2, 3) if topo.die(T.cores[(kr + rank) % N]) != topo.die(core)]
    near = [kr for kr in (1, 2, 3) if kr not in far]

    for t in range(3):
        X = "x%d" % t
        Xn = "x%d" % (t + 1)
        ko = "ko%d" % t
        for r in range(N):
            if t:
                last = R("lr%d" % (t - 1), 128 * r + (rank - r) % N, 128 * r + 128, 4)
            else:
                last = R(X, MB * r + 31, MB * r + MB, 32)
            mm(blk("b4", r, 32), R("bw"), last, True, True)
            act(blk("xrep", r, 32), last, F.Copy)
        mm(R("b0"), R("idf"), R("kc"), True, False)
        for k in range(4):
            mm(blk("b5", k, 32), R("bw"), R(X, 32 * k + 31, 4096, 128), True, True)
        for w in (128, 256, 512):
            act(R("xrep", w, 2 * w), R("xrep", 0, w), F.Copy)
        act(R("wb"), R("jtf", 0, 264), F.Copy, None, 0.0)
        tt(R("mp"), R("b4", 0, 128), MK, A.mult)
        scan(R("sp"), R("rst"), R("mp"), 0.0, A.mult, A.add)
        cp(R("ui"), R("sp", 15, 128, 16))
        ts(R("ub"), R("ui"), 4095, None, A.bitwise_and)
        tt(R("sq"), R("ub"), R("ub"), A.mult)
        cp(R("uf"), R("ub"))
        ts(R("s5"), R("sq"), 5, None, A.arith_shift_right)
        cp(R("u2"), R("s5"))
        for k in range(8):
            ts(R("cv", k, 512, 8), blk("kr", t, 64), R("uf", k, k + 1), R("u2", k, k + 1), A.mult, A.add)
        for a, b in ((0, 128), (128, 512)):
            ts(R("ci", a, b), R("cv", a, b), 4095, None, A.bitwise_and)
            cp(R("cl", a, b), R("ci", a, b))
        ts(R("c16"), R("cl"), -2048.0, None, A.add)

        def gather_s(k):
            m0, m1 = SCH[k]
            act(R("ga", 128 * m0, 128 * m1), R(X), F.Copy, R("cl", 8 * m0, 8 * m1))

        def abs_s(k):
            for c in range(SCH[k][0] // 4, SCH[k][1] // 4):
                bank = R("b%d" % (6 + c % 2))
                mm(bank, R("idb"), blk("ga", c, 512), True, False)
                mm(bank, R("nid"), R("xrep", 0, 512), False, True)
            for c in range(SCH[k][0] // 4, SCH[k][1] // 4):
                act(blk("ab", c, 512), R("b%d" % (6 + c % 2)), F.Abs)

        def dist(m0, m1, stop):
            if m0 >= LATE:
                out = R("b7", 8 * (m0 - LATE), 8 * (m1 - LATE))
            else:
                out = R("b0", 8 * m0, 8 * m1)
            for s in range(16):
                mm(out, blk("ld", s), R("ab", 128 * m0 + s, 128 * m1, 16), False, stop and s == 15)

        e = 8 * LATE
        gather_s(0)
        gather_s(1)
        for k, (m0, m1) in enumerate(VCH):
            tt(R("d", 128 * m0, 128 * m1), R(X), R("xrep", 0, 128 * (m1 - m0)), A.subtract, R("cl", 8 * m0, 8 * m1))
            if k < 2:
                abs_s(k)
            act(R("ab", 128 * m0, 128 * m1), R("d", 128 * m0, 128 * m1), F.Abs)
            if k == 1:
                mm(R("b0"), R("idh"), R("c16"), False, False)
                dist(SCH[0][0], SCH[0][1], False)
                dist(VCH[0][0], VCH[0][1], False)
                dist(SCH[1][0], SCH[1][1], False)
                mm(R("b7", 0, 512 - e), R("idf"), R("kc", e, 512), True, False)
                mm(R("b7", 0, 512 - e), R("idh"), R("c16", e, 512), False, False)
            if 1 <= k and m1 <= LATE:
                dist(m0, m1, m1 == LATE)
        dist(LATE, 64, True)
        if t == 0:
            for j in range(8):
                bank, c, w = SEG[j]
                act(R("ct", CTO[bank] + c, CTO[bank] + c + w), R("ones", 0, w), F.Copy, None, R("tc", j, j + 1))
        for bank, js in BANKS:
            mm(R(bank, 0, BANKW[bank]), R("idf"), R("ct", CTO[bank], CTO[bank] + BANKW[bank]), True, False)
        if t == 0:
            later_constants()
        cp(R("hI"), R("b5", 0, 128))
        ts(R("h63"), R("hI"), 63, None, A.bitwise_and)
        ts(R("hb"), R("ub"), 63, None, A.bitwise_and)
        ts(R("h31"), R("hb"), 1.0, 31.0, A.add, A.mult)
        for bank, a, b in (("b0", 0, e), ("b7", e, 512)):
            tt(R("gd", a, b), R(bank, 0, b - a), R("th2", a, b), A.is_lt)
            tt(R("mk", a, b), R(bank, 0, b - a), R("gd", a, b), A.mult)
        for k in range(8):
            red(R("bf", k, k + 1), R("mk", k, 512, 8), A.min)
        ts(R("dio", 0, 8), R("bf"), 2.0 ** -12, 2047.5 + 2.0 ** -13, A.mult, A.add)
        cp(R("best"), R("bf"))
        ts(R("jI"), R("best"), 5, 127, A.arith_shift_right, A.bitwise_and)
        ts(R("oI"), R("best"), 1, 15, A.arith_shift_right, A.bitwise_and)
        tt(R("jm"), R("jI"), R("il"), A.is_gt)
        tt(R("dio", 8, 16), R("oI"), R("ioc"), A.add)
        tt(R("jv"), R("jI"), R("jm"), A.mult)
        tt(R("ej"), R("jv"), MK, A.mult, E8)
        tt(R("ed"), R("dio"), R("mk2"), A.mult, R("expl"))
        seg = {j: R(SEG[j][0], SEG[j][1], SEG[j][1] + SEG[j][2]) for j in range(8)}
        for bank, js in BANKS:
            for j in js:
                mm(seg[j], R("bo27"), R("ej", 0, SEG[j][2]), False, False)
        for bank, js in BANKS:
            for j in js:
                mm(seg[j], R("bo12"), R("ed", 0, SEG[j][2]), False, False)
                mm(seg[j], R("boh"), R("ed", 128, 128 + SEG[j][2]), False, j == js[-1])
        ts(blk("b0", 0), R("h63"), 1.0, R("pm"), A.add, A.mult)
        ts(blk("b0", 1), R("h63"), 1.0, R("pm16"), A.add, A.mult)
        for bank, js in BANKS:
            for j in js:
                red(R("accf", j, j + 1), seg[j], A.min, True)
        tt(R("acc"), R("accf"), R("self"), A.min)
        ts(R("fI"), R("acc"), 5, 127, A.arith_shift_right, A.bitwise_and)
        ts(R("cI"), R("acc"), 31, None, A.bitwise_and)
        tt(R("ef"), R("fI"), MK, A.mult, E8)
        mm(R("b5", 0, 128), R("bo"), R("ef"), True, True)
        cp(R("fl0"), R("fI"))
        act(R("f0"), R("b5", 0, 128), F.Copy)
        ts(R("lI"), R("cI"), -1.0, 32.0, A.mult, A.add)
        tt(R("el"), R("lI"), MK, A.mult, E8)
        mm(R("b4", 0, 128), R("bo"), R("el"), True, True)
        mm(R("b6"), R("el"), R("grp", 0, 512), True, True)
        mm(R("b7"), R("el"), R("grp", 512, 1024), True, True)
        mm(R("b2"), blk("gsel", 0), R("jt"), True, False)
        mm(R("b3"), blk("gsel", 0), R("jt"), True, False)
        gaps = [
            lambda: red(R("lc"), R("b4", 0, 128), A.add),
            lambda: (ts(R("kl"), R("kperm"), R("lc"), None, A.mult), ts(R("k31"), R("il"), R("lc"), None, A.mult)),
            lambda: (ts(R("sk"), R("kl"), 7, None, A.arith_shift_right),
                     ts(R("s31"), R("k31"), 7, None, A.arith_shift_right)),
            lambda: (tt(R("pp", 0, 256, 2), R("sk"), blk("b0", 0), A.add),
                     tt(R("pp", 1, 256, 2), R("sk"), blk("b0", 1), A.add)),
        ]
        for k in range(4):
            fl = R("fl%d" % k)
            act(R("h%d" % k), R("f%d" % k), F.Copy, fl)
            gaps[k]()
            tt(R("mm"), R("h%d" % k), MK, A.mult, fl)
            act(R("f%d" % (k + 1)), R("h%d" % k), F.Copy, fl)
            act(blk("lb", k, 256), blk("b%d" % (6 + k // 2), k % 2, 256), F.Copy)
            scan(R("sc"), R("rst"), R("mm"), 0.0, A.mult, A.add)
            cp(R("fl%d" % (k + 1)), R("sc", 15, 128, 16))
        tt(R("b6", 0, 128), R("ac"), R("b4", 0, 128), A.subtract)
        mm(R("b4", 0, 8), R("idb"), R("kcol"), True, False)
        act(R("f7"), R("f4"), F.Copy, R("fl4"))
        ts(R("b6", 256, 512), R("pp"), R("lc"), R("lc"), A.is_ge, A.mult)
        tt(R("p31"), R("s31"), R("h31"), A.add)
        tt(R("pw"), R("pp"), R("b6", 256, 512), A.subtract)
        ts(R("w31"), R("p31"), R("lc"), R("lc"), A.is_ge, A.mult)
        mm(R("b4", 0, 8), R("f7"), R("gsel", 0, 1024, 128), False, True)
        act(R("negr", 4, 8), R("b4", 4, 8), F.Copy, None, -1.0)
        order = (4, 5, 6, 7, 0, 1, 2, 3)
        for k in order:
            mm(blk("b2" if k < 4 else "b3", k % 4), blk("gsel", k), R("f7"), False, k % 4 == 3)
        for k in range(4, 8):
            mm(R("b5", 0, 128), blk("lb", k), R("omi"), k == 4, False)
        for k in order:
            if k < 4:
                ts(blk("cmp", k), blk("b2", k), R("b4", k, k + 1), None, A.is_gt)
            else:
                act(blk("cmp", k), blk("b3", k % 4), F.Sign, None, None, R("negr", k, k + 1))
        for k in (0, 1, 4, 5, 2, 3, 6, 7):
            mm(R("b5", 0, 128), blk("lb", k), blk("cmp", k), False, k == 7)
        tt(R("q31"), R("p31"), R("w31"), A.subtract)
        cp(R("plist"), R("pw"))
        cp(R("l31"), R("q31"))
        tt(R("mp"), R("b5", 0, 128), MK, A.mult)
        act(R("t4"), R("b5", 0, 128), F.Copy, None, 4095.0)
        scan(R("sp"), R("rst"), R("mp"), 0.0, A.mult, A.add)
        ts(R("cell"), R("sp", 15, 128, 16), 0.0625, -0.46875, A.mult, A.add)
        tt(R("vrow"), R("t4"), R("b6", 0, 128), A.add)
        cp(R("celll"), R("cell"))
        cp(R("wb", 8, 264), R("vrow"), None, R("celll"))

        def step(n, a, b):
            if n == 0:
                tt(R("b7", a, b), R("wb", 8 + a, 8 + b), R("b1", a, b), A.is_lt)
            elif n == 1:
                tt(R("w1", a, b), R("wb", 8 + a, 8 + b), R("b7", a, b), A.mult)
            elif n == 2:
                scan(R("ff", a, b), R("wb", 7 + a, 7 + b), R("w1", a, b), R("ff", a - 1, a) if a else 0.0, A.max, A.max)
            elif n == 3:
                tt(R("si", a, b), R("ff", a, b), R("b1", 256 + a, 256 + b), A.add)
            elif n == 4:
                ts(R("sj", a, b), R("si", a, b), 4095, None, A.bitwise_and)
            else:
                cp(R("sl", a, b), R("sj", a, b))
        for n, second in ((0, 0), (0, 1), (1, 0), (1, 1), (2, 0), (3, 0), (2, 1), (4, 0), (3, 1), (5, 0), (4, 1), (5, 1)):
            if second:
                step(n, LAYS, 256)
            else:
                step(n, 0, LAYS)
        act(R("lay", 0, 16 * LAYS), R(X), F.Copy, R("sl", 0, LAYS))
        cp(R("lay", 16 * LAYS, 4096), R(X), R("sl", LAYS, 256))
        to = blk(Xn, rank, MB)

        def kids(q, kr, a, b):
            buf, o = (ko, MB * (kr - 1)) if kr else (Xn, MB * rank)
            lst = R("plist", 64 * kr + a, 64 * kr + b)
            if q == "V":
                cp(R(buf, o + 16 * a, o + 16 * b), R("lay"), lst)
            else:
                act(R(buf, o + 16 * a, o + 16 * b), R("lay"), F.Copy, lst)

        def send(krs, buf, into, rs, ls):
            dsts = [T.cores[(kr + rank) % N] for kr in krs]
            ids = [DstId(rid=topo.addr(dst)[0], pnc=topo.addr(dst)[1]) for dst in dsts]
            sync("G", [], [buf])
            g.remote_dma_fused([RemoteDMATransfer(dst_ids=ids, dma_engine_mask=topo.mask(core, dsts[0]), srcs=[ap(buf)],
                                                  dsts=[ap(into) for _ in krs], remote_sem=T.sem[rs])],
                               local_sem=T.sem[ls])
        if t < 2:
            lr = "lr%d" % t
            cp(blk(lr, rank), R("lay"), R("l31"))
            send((1, 2, 3), blk(lr, rank), blk(lr, rank), "sm%d" % t, "lq%d" % t)
            arrive("sm%d" % t, 3 * ne, [blk(lr, r) for r in range(N) if r != rank])
            extra.append(("lq%d" % t, ne))
        for kr in far + near + [0]:
            kids("V", kr, 0, 32)
            kids("S", kr, 32, 64)
            if kr:
                send((kr,), blk(ko, kr - 1, MB), to, "ar%d_%d" % (t, kr), "ls%d" % t)
        extra.append(("ls%d" % t, 3 * ne))
        for kr in (1, 2, 3):
            arrive("ar%d_%d" % (t, kr), ne, [blk(Xn, (rank - kr) % N, MB)])
    for kr in [0] + [(-k) % N for k in far + near]:
        s = (rank - kr) % N
        dma("Y", T.y[:, MB * s:MB * s + MB], T.x3[:, MB * s:MB * s + MB], [], [blk("x3", s, MB)])
    finish(extra)
